import numpy as np
import ml_dtypes


def mxq(x, axis, fmt="e4m3"):
    dtype, down = {"e4m3": (ml_dtypes.float8_e4m3fn, 7), "e5m2": (ml_dtypes.float8_e5m2, 14)}[fmt]
    v = np.moveaxis(np.asarray(x, np.float32).astype(ml_dtypes.bfloat16).astype(np.float64), axis, -1)
    blocks = v.reshape(v.shape[:-1] + (-1, 32))
    amax = np.abs(blocks).max(-1, keepdims=True)
    byte = np.maximum(np.where(amax > 0, np.frexp(amax)[1] - 1 + 127, 0) - down, 1)
    scale = np.exp2(byte - 127.0)
    codes = (blocks / scale).astype(np.float32).astype(dtype).astype(np.float64)
    return np.moveaxis((codes * scale).reshape(v.shape), -1, axis)


WIDE = False


def mx_kscale(k):
    if not WIDE:
        return np.ones(k)
    levels = np.array([10, -10, 5, -5, 0])
    if k % 512:
        return np.exp2(np.random.permutation(np.resize(levels, k // 32))).repeat(32)
    a = np.empty((k // 512, 16))
    for p in range(k // 512):
        a[p, :8] = np.random.permutation(np.resize(levels, 8))
        for g in range(8):
            far = levels[np.abs(levels - a[p, g]) >= 10]
            a[p, g + 8] = far[np.random.randint(len(far))]
    return np.exp2(a.ravel()).repeat(32)


BF16 = ml_dtypes.bfloat16


def bf(x):
    return np.asarray(x, np.float32).astype(BF16)


def f64(x):
    return np.asarray(x).astype(np.float64)


E2M1 = np.array([0.0, 0.5, 1.0, 1.5, 2.0, 3.0, 4.0, 6.0, -0.0, -0.5, -1.0, -1.5, -2.0, -3.0, -4.0, -6.0])


def pack_weight(w, fmt):
    k, n = w.shape
    w = f64(bf(w)).reshape(k // 32, 32, n)
    amax = np.abs(w).max(1)
    if fmt == "e4m3":
        byte = np.frexp(amax)[1] - 1 + 127 - 7
    else:
        mant, ex = np.frexp(amax / 6.0)
        byte = np.where(mant > 0.5, ex, ex - 1) + 127
    byte = np.clip(np.where(amax > 0, byte, 1), 1, 254)
    scaled = (w * np.exp2(127.0 - byte)[:, None, :]).reshape(k, n).astype(np.float32)
    by_word = np.ascontiguousarray(scaled.reshape(k // 512, 128, 4, n).transpose(0, 1, 3, 2))
    if fmt == "e4m3":
        words = by_word.astype(ml_dtypes.float8_e4m3fn).view(np.uint8)
    else:
        c = by_word.astype(ml_dtypes.float4_e2m1fn).view(np.uint8) & 0xF
        words = c[..., 0::2] | (c[..., 1::2] << 4)
    return np.ascontiguousarray(words), np.ascontiguousarray(byte.astype(np.uint8).reshape(k // 512, 16, n))


def unpack_weight(words, scales, fmt):
    g, p, n, _ = words.shape
    if fmt == "e4m3":
        vals = np.ascontiguousarray(words).view(ml_dtypes.float8_e4m3fn).astype(np.float64)
    else:
        nib = np.empty((g, p, n, 4), np.uint8)
        nib[..., 0::2] = words & 0xF
        nib[..., 1::2] = words >> 4
        vals = E2M1[nib]
    vals = vals * np.repeat(np.exp2(scales.astype(np.float64) - 127.0), 8, axis=1)[..., None]
    return vals.transpose(0, 1, 3, 2).reshape(g * 512, n)

E4M3FN = np.array([(-1.0 if i & 128 else 1.0) * ((1.0 + (i & 7) / 8.0) * 2.0 ** (((i >> 3) & 15) - 7) if i & 120 else (i & 7) * 2.0 ** -9) for i in range(256)])


def e4m3fn_bytes(y):
    return np.clip(np.asarray(y, np.float64), -448.0, 448.0).astype(np.float32).astype(ml_dtypes.float8_e4m3fn).view(np.uint8)


def e4m3fn_values(b):
    return E4M3FN[b]


S, P, M = 1024, 512, 1024


def draw0():
    a, c = mx_kscale(S), mx_kscale(P)
    r = bf(np.random.standard_normal((S, M)) * a[:, None])
    v = bf(np.random.standard_normal((P, M)) * c[:, None])
    finv = bf(np.random.uniform(0.5, 1.5, P))
    k_words, k_scales = pack_weight(np.random.standard_normal((S, P)) / np.sqrt(S) / a[:, None] * c[None, :], "e4m3")
    z_words, z_scales = pack_weight(np.random.standard_normal((P, S)) / np.sqrt(P) / c[:, None], "e4m3")
    t_words, t_scales = pack_weight(np.random.standard_normal((S, S)) / np.sqrt(S) / a[:, None], "e4m3")
    h = bf(np.random.uniform(0.5, 1.5, P) / c)
    return {
        "r": r,
        "v": v,
        "finv": finv,
        "k_words": k_words,
        "k_scales": k_scales,
        "z_words": z_words,
        "z_scales": z_scales,
        "t_words": t_words,
        "t_scales": t_scales,
        "h": h,
    }


def core(r, v, finv, k_words, k_scales, z_words, z_scales, t_words, t_scales, h):
    rq = mxq(f64(r), 0, "e4m3")
    kr = unpack_weight(k_words, k_scales, "e4m3").T @ rq
    u = f64(finv)[:, None] * f64(v) - kr
    zu = unpack_weight(z_words, z_scales, "e4m3").T @ mxq(u, 0, "e4m3")
    tr = unpack_weight(t_words, t_scales, "e4m3").T @ rq
    r_prev = zu + tr
    eps = f64(h)[:, None] * u
    return r_prev, eps


def setup_inputs():
    drawn = draw0()
    full = np.asarray(drawn['r']).astype(np.float64)
    scale = (np.abs(full).reshape(1024, 8, 128).max(axis=(2,)) / 448.0).astype(np.float32)
    given = {}
    for key, value in drawn.items():
        if key == 'r':
            given['r_bytes'] = e4m3fn_bytes(full / np.repeat(scale.astype(np.float64), 128, axis=1))
            given['r_scale'] = scale
        else:
            given[key] = value
    return given


def reference(r_bytes, r_scale, v, finv, k_words, k_scales, z_words, z_scales, t_words, t_scales, h):
    return core(e4m3fn_values(r_bytes) * np.repeat(r_scale.astype(np.float64), 128, axis=1), v, finv, k_words, k_scales, z_words, z_scales, t_words, t_scales, h)

@@ -1,0 +1,359 @@
+from contextlib import ExitStack
+
+import concourse.mybir as mybir
+
+S, P_OBS, M = 1024, 512, 1024
+FLOPS = 2 * M * (2 * S * P_OBS + S * S)
+
+F32 = mybir.dt.float32
+BF16 = mybir.dt.bfloat16
+I32 = mybir.dt.int32
+U32 = mybir.dt.uint32
+U8 = mybir.dt.uint8
+FP8 = mybir.dt.float8_e4m3fn
+FP8X4 = mybir.dt.float8_e4m3fn_x4
+COPY = mybir.ActivationFunctionType.Copy
+MULT = mybir.AluOpType.mult
+SUB = mybir.AluOpType.subtract
+
+P = 128
+PACK = 4
+BLOCK = 128
+BANK = 512
+
+GROUPS = ((256,), (256,), (256,), (256,))
+SLICES = (2, 2, 2, 1)
+
+
+def tile_durbinkoopmandisturbancesmootherstep_d1p_kernel(
+    tc, r_bytes, r_scale, v, finv, k_words, k_scales, z_words, z_scales, t_words, t_scales, h, out_0, out_1
+):
+    nc = tc.nc
+    chunks = []
+    group_start, group_width = [], []
+    at = 0
+    for gi, parts in enumerate(GROUPS):
+        group_start.append(at)
+        group_width.append(sum(parts))
+        off = 0
+        for w in parts:
+            chunks.append((gi, off, w, at))
+            off += w
+            at += w
+    n_chunks = len(chunks)
+
+    r_view = r_bytes.rearrange("(g p t) m -> p g t m", p=P, t=PACK)
+    v_view = v.rearrange("(p t) m -> p t m", t=PACK)
+    eps_view = out_1.rearrange("(p t) m -> p t m", t=PACK)
+    prev_view = out_0.rearrange("(s p) m -> p s m", p=P)
+
+    with ExitStack() as ctx:
+        keep = ctx.enter_context(tc.tile_pool(name="keep", bufs=1))
+        psum = ctx.enter_context(tc.psum_pool(name="psum", bufs=8))
+        ctx.enter_context(tc.manual_schedule())
+
+        r_raw = keep.tile([P, 2, PACK, M], U8, name="r_raw", align_bytes=256)
+        r_sc = keep.tile([P, 2, PACK, M // BLOCK], F32, name="r_sc", align_bytes=256)
+        v_sb = keep.tile([P, PACK, M], BF16, name="v_sb", align_bytes=256)
+        vec_bf = keep.tile([P, 2, 16], BF16, name="vec_bf", align_bytes=256)
+        vec = keep.tile([P, 2, PACK], F32, name="vec", align_bytes=256)
+        k_raw = keep.tile([P, 2, P_OBS], U32, name="k_raw", align_bytes=256)
+        k_codes = keep.tile([P, 2, P_OBS], U32, name="k_codes", align_bytes=256)
+        ks_raw = keep.tile([P, P_OBS], U8, name="ks_raw", align_bytes=256)
+        k_sc = keep.tile([P, P_OBS], U8, name="k_sc", align_bytes=256)
+        t_codes = keep.tile([P, 2, S], U32, name="t_codes", align_bytes=256)
+        z_codes = keep.tile([P, S], U32, name="z_codes", align_bytes=256)
+        t_sc = keep.tile([P, S], U8, name="t_sc", align_bytes=256)
+        z_sc = keep.tile([P, S], U8, name="z_sc", align_bytes=256)
+
+        for plane in (ks_raw, t_sc, z_sc):
+            nc.vector.memset(plane[:].bitcast(U32), 0)
+        k_dram = k_words.rearrange("g p n t -> p g (n t)").bitcast(I32)
+        t_dram = t_words.rearrange("g p n t -> p g (n t)").bitcast(I32)
+        z_dram = z_words[0].rearrange("p n t -> p (n t)").bitcast(I32)
+
+        def load_ks(queue, q):
+            queue.dma_start(
+                out=ks_raw[32 * q : 32 * q + 8, :].bitcast(I32), in_=k_scales[:, 4 * q : 4 * q + 4, :].bitcast(I32)
+            )
+
+        def load_ts(queue, q):
+            queue.dma_start(
+                out=t_sc[32 * q : 32 * q + 8, :].bitcast(I32), in_=t_scales[:, 4 * q : 4 * q + 4, :].bitcast(I32)
+            )
+
+        def load_zs(queue, q):
+            queue.dma_start(
+                out=z_sc[32 * q : 32 * q + 4, :].bitcast(I32), in_=z_scales[0, 4 * q : 4 * q + 4, :].bitcast(I32)
+            )
+
+        def load_vec(queue, i, src):
+            queue.dma_start(out=vec_bf[:, i, 0:PACK], in_=src.rearrange("(p t) -> p t", t=PACK))
+
+        nc.sync.dma_start(out=r_sc[:], in_=r_scale.rearrange("(g p t) j -> p g t j", p=P, t=PACK))
+        nc.sync.dma_start(out=r_raw[:, 0], in_=r_view[:, 0])
+        for q in range(4):
+            load_ks(nc.sync, q)
+        nc.sync.dma_start(out=r_raw[:, 1], in_=r_view[:, 1])
+        nc.sync.dma_start(out=k_raw[:].bitcast(I32), in_=k_dram)
+        nc.sync.dma_start(out=t_codes[:].bitcast(I32), in_=t_dram)
+        load_vec(nc.scalar, 0, finv)
+        for q in range(4):
+            load_ts(nc.sync, q)
+        nc.sync.dma_start(out=v_sb[:, :, 0:512], in_=v_view[:, :, 0:512])
+        nc.sync.dma_start(out=z_codes[:].bitcast(I32), in_=z_dram)
+        load_vec(nc.sync, 1, h)
+        for q in range(4):
+            load_zs(nc.sync, q)
+        nc.sync.dma_start(out=v_sb[:, :, 512:1024], in_=v_view[:, :, 512:1024])
+
+        wide, mixed, r_codes, r_planes = {}, {}, [], []
+        u32, u_mixed, u_codes, u_planes, eps = [], {}, [], [], []
+        for gi, w in enumerate(group_width):
+            r_codes.append(keep.tile([P, 2, w], U32, name="r_codes%d" % gi, align_bytes=256))
+            r_planes.append(keep.tile([P, 2, w], U8, name="r_planes%d" % gi, align_bytes=256))
+            u32.append(keep.tile([P, PACK, w], F32, name="u32_%d" % gi, align_bytes=256))
+            u_codes.append(keep.tile([P, w], U32, name="u_codes%d" % gi, align_bytes=256))
+            u_planes.append(keep.tile([P, w], U8, name="u_planes%d" % gi, align_bytes=256))
+            eps.append(keep.tile([P, PACK, w], F32, name="eps%d" % gi, align_bytes=256))
+        for f, (gi, off, w, lo) in enumerate(chunks):
+            u_mixed[f] = keep.tile([P, w, PACK], BF16, name="u_mixed%d" % f, align_bytes=256)
+            for g in range(2):
+                wide[f, g] = keep.tile([P, PACK, w], BF16, name="wide%d_%d" % (f, g), align_bytes=256)
+                mixed[f, g] = keep.tile([P, w, PACK], BF16, name="mixed%d_%d" % (f, g), align_bytes=256)
+
+        def W(f, g, engine="s", ts=(0, 1, 2, 3)):
+            gi, off, w, lo = chunks[f]
+            for t in ts:
+                for b in range(w // BLOCK):
+                    col = lo + b * BLOCK
+                    src = r_raw[:, g, t, col : col + BLOCK].bitcast(FP8)
+                    dst = wide[f, g][:, t, b * BLOCK : (b + 1) * BLOCK]
+                    sc = r_sc[:, g, t, col // BLOCK : col // BLOCK + 1]
+                    if engine == "v":
+                        nc.vector.tensor_scalar(out=dst, in0=src, scalar1=sc, scalar2=None, op0=MULT)
+                    else:
+                        nc.scalar.activation(out=dst, in_=src, func=COPY, scale=sc)
+
+        def Mx(f, g, engine="v"):
+            dst = mixed[f, g][:].rearrange("p (c i) t -> p c t i", i=4)
+            src = wide[f, g][:].rearrange("p t (c i) -> p c t i", i=4)
+            if engine == "v":
+                nc.vector.tensor_copy(out=dst, in_=src)
+            else:
+                nc.scalar.copy(out=dst, in_=src)
+
+        def Q(f, g):
+            gi, off, w, lo = chunks[f]
+            nc.vector.quantize_mx(
+                out=r_codes[gi][:, g, off : off + w].bitcast(FP8X4),
+                scales=r_planes[gi][:, g, off : off + w],
+                in_=mixed[f, g][:].rearrange("p n t -> p (n t)"),
+            )
+
+        def KS():
+            nc.vector.tensor_copy(
+                out=k_sc[:].rearrange("p (t m) -> p t m", t=PACK), in_=ks_raw[:].rearrange("p (m t) -> p t m", t=PACK)
+            )
+
+        def KW(half):
+            nc.vector.tensor_copy(
+                out=k_codes[:].bitcast(I32).rearrange("p g (t m) -> p g t m", t=PACK)[:, :, 2 * half : 2 * half + 2, :],
+                in_=k_raw[:].bitcast(I32).rearrange("p g (m t) -> p g t m", t=PACK)[:, :, 2 * half : 2 * half + 2, :],
+            )
+
+        def VEC(i):
+            nc.vector.tensor_copy(out=vec[:, i, :], in_=vec_bf[:, i, 0:PACK])
+
+        kr = {}
+
+        def K(f):
+            gi, off, w, lo = chunks[f]
+            per = BANK // w
+            for b in range(PACK // per):
+                bank = psum.tile([P, per, w], F32, name="bank")
+                kr[f, b] = bank
+                for i in range(per):
+                    cols = slice((b * per + i) * P, (b * per + i + 1) * P)
+                    for g in range(2):
+                        nc.tensor.matmul_mx(
+                            out=bank[:, i, :],
+                            lhsT=k_codes[:, g, cols].bitcast(FP8X4),
+                            lhsT_scale=k_sc[4 * g : P, cols],
+                            rhs=r_codes[gi][:, g, off : off + w].bitcast(FP8X4),
+                            rhs_scale=r_planes[gi][:, g, off : off + w],
+                            start=(g == 0),
+                            stop=(g == 1),
+                        )
+
+        def U(f):
+            gi, off, w, lo = chunks[f]
+            per = BANK // w
+            for t in range(PACK):
+                nc.vector.scalar_tensor_tensor(
+                    out=u32[gi][:, t, off : off + w],
+                    in0=v_sb[:, t, lo : lo + w],
+                    scalar=vec[:, 0, t : t + 1],
+                    in1=kr[f, t // per][:, t % per, :],
+                    op0=MULT,
+                    op1=SUB,
+                )
+
+        def J(f):
+            gi, off, w, lo = chunks[f]
+            nc.vector.tensor_copy(out=u_mixed[f][:], in_=u32[gi][:, :, off : off + w].rearrange("p t n -> p n t"))
+
+        def Pq(f):
+            gi, off, w, lo = chunks[f]
+            nc.vector.quantize_mx(
+                out=u_codes[gi][:, off : off + w].bitcast(FP8X4),
+                scales=u_planes[gi][:, off : off + w],
+                in_=u_mixed[f][:].rearrange("p n t -> p (n t)"),
+            )
+
+        def E(f, ts, engine):
+            gi, off, w, lo = chunks[f]
+            for t in ts:
+                src, dst = u32[gi][:, t, off : off + w], eps[gi][:, t, off : off + w]
+                if engine == "v":
+                    nc.vector.tensor_scalar(out=dst, in0=src, scalar1=vec[:, 1, t : t + 1], scalar2=None, op0=MULT)
+                else:
+                    nc.scalar.activation(out=dst, in_=src, func=COPY, scale=vec[:, 1, t : t + 1])
+
+        def store_eps(gi):
+            nc.sync.dma_start(
+                out=eps_view[:, :, group_start[gi] : group_start[gi] + group_width[gi]], in_=eps[gi][:]
+            )
+
+        acc = {}
+
+        def open_bank(gi, b):
+            acc[gi, b] = psum.tile([P, SLICES[gi], group_width[gi]], F32, name="bank")
+
+        def transition(gi, b, i):
+            s = b * SLICES[gi] + i
+            cols = slice(s * P, (s + 1) * P)
+            for g in range(2):
+                nc.tensor.matmul_mx(
+                    out=acc[gi, b][:, i, :],
+                    lhsT=t_codes[:, g, cols].bitcast(FP8X4),
+                    lhsT_scale=t_sc[4 * g : P, cols],
+                    rhs=r_codes[gi][:, g, :].bitcast(FP8X4),
+                    rhs_scale=r_planes[gi][:, g, :],
+                    start=(g == 0),
+                    stop=False,
+                )
+
+        def observe(gi, b, i):
+            s = b * SLICES[gi] + i
+            cols = slice(s * P, (s + 1) * P)
+            nc.tensor.matmul_mx(
+                out=acc[gi, b][:, i, :],
+                lhsT=z_codes[:, cols].bitcast(FP8X4),
+                lhsT_scale=z_sc[:, cols],
+                rhs=u_codes[gi][:].bitcast(FP8X4),
+                rhs_scale=u_planes[gi][:],
+                start=False,
+                stop=True,
+            )
+
+        def T(gi, banks):
+            for b in banks:
+                open_bank(gi, b)
+                transition(gi, b, 0)
+
+        def O(gi, banks, engines):
+            for b, engine in zip(banks, engines):
+                if (gi, b) not in acc:
+                    open_bank(gi, b)
+                    transition(gi, b, 0)
+                observe(gi, b, 0)
+                for i in range(1, SLICES[gi]):
+                    transition(gi, b, i)
+                    observe(gi, b, i)
+                per, w, lo = SLICES[gi], group_width[gi], group_start[gi]
+                res = keep.tile([P, per, w], F32, name="res%d_%d" % (gi, b), align_bytes=256)
+                if engine == "v":
+                    nc.vector.tensor_copy(out=res[:], in_=acc[gi, b][:])
+                else:
+                    nc.scalar.copy(out=res[:], in_=acc[gi, b][:])
+                nc.sync.dma_start(out=prev_view[:, b * per : (b + 1) * per, lo : lo + w], in_=res[:])
+
+        def WARM(n):
+            bank = psum.tile([P, BANK], F32, name="bank")
+            src = wide[0, 0]
+            for i in range(n):
+                nc.tensor.matmul(
+                    bank[:],
+                    lhsT=src[:, 0, 0:P],
+                    rhs=src[:, 0:2, :].rearrange("p t n -> p (t n)"),
+                    start=True,
+                    stop=True,
+                )
+
+        W(0, 0, "v", (0, 1))
+        W(0, 0, "s", (2, 3))
+        WARM(8)
+        W(1, 0, "s", (0, 1))
+        Mx(0, 0)
+        KS()
+        W(0, 1, "s", (0, 1))
+        W(0, 1, "v", (2, 3))
+        Q(0, 0)
+        Mx(0, 1)
+        W(1, 0, "s", (2, 3))
+        W(1, 1)
+        W(2, 0)
+        W(2, 1)
+        KW(0)
+        Q(0, 1)
+        KW(1)
+        K(0)
+        T(0, range(4))
+        VEC(0)
+        Mx(1, 0)
+        Mx(1, 1)
+        Q(1, 0)
+        Q(1, 1)
+        K(1)
+        U(0)
+        VEC(1)
+        W(3, 0)
+        J(0)
+        E(0, (0, 1, 2, 3), "s")
+        store_eps(0)
+        W(3, 1)
+        T(1, range(2))
+        Pq(0)
+        O(0, range(4), "ssss")
+        Mx(2, 0)
+        Mx(2, 1)
+        U(1)
+        Q(2, 0)
+        Q(2, 1)
+        K(2)
+        J(1)
+        E(1, (0, 1, 2, 3), "s")
+        store_eps(1)
+        Pq(1)
+        T(1, range(2, 3))
+        O(1, range(4), "ssss")
+        Mx(3, 0)
+        Mx(3, 1)
+        U(2)
+        Q(3, 0)
+        Q(3, 1)
+        T(2, range(2))
+        K(3)
+        J(2)
+        E(2, (0, 1, 2, 3), "s")
+        store_eps(2)
+        Pq(2)
+        O(2, range(4), "ssss")
+        U(3)
+        J(3)
+        Pq(3)
+        E(3, (0, 1), "s")
+        E(3, (2, 3), "v")
+        store_eps(3)
+        O(3, range(8), "vsvsvsvs")

@@ -19,29 +19,14 @@ SUB = mybir.AluOpType.subtract
 P = 128
 PACK = 4
 BLOCK = 128
-BANK = 512
-
-GROUPS = ((256,), (256,), (256,), (256,))
-SLICES = (2, 2, 2, 1)
+W = 256
+CHUNKS = M // W
 
 
 def tile_durbinkoopmandisturbancesmootherstep_d1p_kernel(
     tc, r_bytes, r_scale, v, finv, k_words, k_scales, z_words, z_scales, t_words, t_scales, h, out_0, out_1
 ):
     nc = tc.nc
-    chunks = []
-    group_start, group_width = [], []
-    at = 0
-    for gi, parts in enumerate(GROUPS):
-        group_start.append(at)
-        group_width.append(sum(parts))
-        off = 0
-        for w in parts:
-            chunks.append((gi, off, w, at))
-            off += w
-            at += w
-    n_chunks = len(chunks)
-
     r_view = r_bytes.rearrange("(g p t) m -> p g t m", p=P, t=PACK)
     v_view = v.rearrange("(p t) m -> p t m", t=PACK)
     eps_view = out_1.rearrange("(p t) m -> p t m", t=PACK)
@@ -49,311 +34,301 @@ def tile_durbinkoopmandisturbancesmootherstep_d1p_kernel(
 
     with ExitStack() as ctx:
         keep = ctx.enter_context(tc.tile_pool(name="keep", bufs=1))
-        psum = ctx.enter_context(tc.psum_pool(name="psum", bufs=8))
+        k_psum = ctx.enter_context(tc.psum_pool(name="k_psum", bufs=2))
+        o_psum = ctx.enter_context(tc.psum_pool(name="o_psum", bufs=6))
         ctx.enter_context(tc.manual_schedule())
 
-        r_raw = keep.tile([P, 2, PACK, M], U8, name="r_raw", align_bytes=256)
-        r_sc = keep.tile([P, 2, PACK, M // BLOCK], F32, name="r_sc", align_bytes=256)
-        v_sb = keep.tile([P, PACK, M], BF16, name="v_sb", align_bytes=256)
-        vec_bf = keep.tile([P, 2, 16], BF16, name="vec_bf", align_bytes=256)
-        vec = keep.tile([P, 2, PACK], F32, name="vec", align_bytes=256)
-        k_raw = keep.tile([P, 2, P_OBS], U32, name="k_raw", align_bytes=256)
-        k_codes = keep.tile([P, 2, P_OBS], U32, name="k_codes", align_bytes=256)
-        ks_raw = keep.tile([P, P_OBS], U8, name="ks_raw", align_bytes=256)
-        k_sc = keep.tile([P, P_OBS], U8, name="k_sc", align_bytes=256)
-        t_codes = keep.tile([P, 2, S], U32, name="t_codes", align_bytes=256)
-        z_codes = keep.tile([P, S], U32, name="z_codes", align_bytes=256)
-        t_sc = keep.tile([P, S], U8, name="t_sc", align_bytes=256)
-        z_sc = keep.tile([P, S], U8, name="z_sc", align_bytes=256)
+        def sbuf(name, shape, dtype):
+            return keep.tile(shape, dtype, name=name, align_bytes=256)
 
-        for plane in (ks_raw, t_sc, z_sc):
-            nc.vector.memset(plane[:].bitcast(U32), 0)
+        r_raw = [sbuf("r_raw%d" % g, [P, PACK, M], U8) for g in range(2)]
+        r_sc = sbuf("r_sc", [P, 2, PACK, M // BLOCK], F32)
+        v_sb = sbuf("v_sb", [P, PACK, M], BF16)
+        finv_bf = sbuf("finv_bf", [P, PACK], BF16)
+        h_bf = sbuf("h_bf", [P, PACK], BF16)
+        h_f32 = sbuf("h_f32", [P, PACK], F32)
+        k_raw = sbuf("k_raw", [P, 2, P_OBS], U32)
+        k_codes = sbuf("k_codes", [P, 2, P_OBS], U32)
+        ks_raw = sbuf("ks_raw", [P, P_OBS], U8)
+        k_sc = sbuf("k_sc", [P, P_OBS], U8)
+        t_codes = [sbuf("t_codes%d" % g, [P, S], U32) for g in range(2)]
+        z_codes = sbuf("z_codes", [P, S], U32)
+        t_sc = sbuf("t_sc", [P, S], U8)
+        z_sc = sbuf("z_sc", [P, S], U8)
+
+        wide, mixed, r_codes, r_planes = {}, {}, {}, {}
+        u32, u_mixed, u_codes, u_planes, eps, res = {}, {}, {}, {}, {}, {}
+        for f in range(CHUNKS):
+            u32[f] = sbuf("u32_%d" % f, [P, PACK, W], F32)
+            u_mixed[f] = sbuf("u_mixed%d" % f, [P, W, PACK], BF16)
+            u_codes[f] = sbuf("u_codes%d" % f, [P, W], U32)
+            u_planes[f] = sbuf("u_planes%d" % f, [P, W], U8)
+            eps[f] = sbuf("eps%d" % f, [P, PACK, W], F32)
+            res[f] = sbuf("res%d" % f, [P, S // P, W], F32)
+            for g in range(2):
+                wide[f, g] = sbuf("wide%d_%d" % (f, g), [P, PACK, W], BF16)
+                mixed[f, g] = sbuf("mixed%d_%d" % (f, g), [P, W, PACK], BF16)
+                r_codes[f, g] = sbuf("r_codes%d_%d" % (f, g), [P, W], U32)
+                r_planes[f, g] = sbuf("r_planes%d_%d" % (f, g), [P, W], U8)
+
         k_dram = k_words.rearrange("g p n t -> p g (n t)").bitcast(I32)
-        t_dram = t_words.rearrange("g p n t -> p g (n t)").bitcast(I32)
+        t_dram = t_words.rearrange("g p n t -> g p (n t)").bitcast(I32)
         z_dram = z_words[0].rearrange("p n t -> p (n t)").bitcast(I32)
 
-        def load_ks(queue, q):
-            queue.dma_start(
-                out=ks_raw[32 * q : 32 * q + 8, :].bitcast(I32), in_=k_scales[:, 4 * q : 4 * q + 4, :].bitcast(I32)
-            )
+        def load_planes(plane, scales, groups):
+            for q in range(4):
+                nc.sync.dma_start(
+                    out=plane[32 * q : 32 * q + 4 * groups, :].bitcast(I32),
+                    in_=scales[:, 4 * q : 4 * q + 4, :].bitcast(I32),
+                )
 
-        def load_ts(queue, q):
-            queue.dma_start(
-                out=t_sc[32 * q : 32 * q + 8, :].bitcast(I32), in_=t_scales[:, 4 * q : 4 * q + 4, :].bitcast(I32)
-            )
+        def load_v(lo, hi):
+            nc.sync.dma_start(out=v_sb[:, :, lo:hi], in_=v_view[:, :, lo:hi])
 
-        def load_zs(queue, q):
-            queue.dma_start(
-                out=z_sc[32 * q : 32 * q + 4, :].bitcast(I32), in_=z_scales[0, 4 * q : 4 * q + 4, :].bitcast(I32)
-            )
+        def widen(f, g, engine, blocks):
+            for i in blocks:
+                t, b = divmod(i, W // BLOCK)
+                col = f * W + b * BLOCK
+                src = r_raw[g][:, t, col : col + BLOCK].bitcast(FP8)
+                dst = wide[f, g][:, t, b * BLOCK : (b + 1) * BLOCK]
+                sc = r_sc[:, g, t, col // BLOCK : col // BLOCK + 1]
+                if engine == "v":
+                    nc.vector.tensor_scalar(out=dst, in0=src, scalar1=sc, scalar2=None, op0=MULT)
+                else:
+                    nc.scalar.activation(out=dst, in_=src, func=COPY, scale=sc)
 
-        def load_vec(queue, i, src):
-            queue.dma_start(out=vec_bf[:, i, 0:PACK], in_=src.rearrange("(p t) -> p t", t=PACK))
-
-        nc.sync.dma_start(out=r_sc[:], in_=r_scale.rearrange("(g p t) j -> p g t j", p=P, t=PACK))
-        nc.sync.dma_start(out=r_raw[:, 0], in_=r_view[:, 0])
-        for q in range(4):
-            load_ks(nc.sync, q)
-        nc.sync.dma_start(out=r_raw[:, 1], in_=r_view[:, 1])
-        nc.sync.dma_start(out=k_raw[:].bitcast(I32), in_=k_dram)
-        nc.sync.dma_start(out=t_codes[:].bitcast(I32), in_=t_dram)
-        load_vec(nc.scalar, 0, finv)
-        for q in range(4):
-            load_ts(nc.sync, q)
-        nc.sync.dma_start(out=v_sb[:, :, 0:512], in_=v_view[:, :, 0:512])
-        nc.sync.dma_start(out=z_codes[:].bitcast(I32), in_=z_dram)
-        load_vec(nc.sync, 1, h)
-        for q in range(4):
-            load_zs(nc.sync, q)
-        nc.sync.dma_start(out=v_sb[:, :, 512:1024], in_=v_view[:, :, 512:1024])
-
-        wide, mixed, r_codes, r_planes = {}, {}, [], []
-        u32, u_mixed, u_codes, u_planes, eps = [], {}, [], [], []
-        for gi, w in enumerate(group_width):
-            r_codes.append(keep.tile([P, 2, w], U32, name="r_codes%d" % gi, align_bytes=256))
-            r_planes.append(keep.tile([P, 2, w], U8, name="r_planes%d" % gi, align_bytes=256))
-            u32.append(keep.tile([P, PACK, w], F32, name="u32_%d" % gi, align_bytes=256))
-            u_codes.append(keep.tile([P, w], U32, name="u_codes%d" % gi, align_bytes=256))
-            u_planes.append(keep.tile([P, w], U8, name="u_planes%d" % gi, align_bytes=256))
-            eps.append(keep.tile([P, PACK, w], F32, name="eps%d" % gi, align_bytes=256))
-        for f, (gi, off, w, lo) in enumerate(chunks):
-            u_mixed[f] = keep.tile([P, w, PACK], BF16, name="u_mixed%d" % f, align_bytes=256)
-            for g in range(2):
-                wide[f, g] = keep.tile([P, PACK, w], BF16, name="wide%d_%d" % (f, g), align_bytes=256)
-                mixed[f, g] = keep.tile([P, w, PACK], BF16, name="mixed%d_%d" % (f, g), align_bytes=256)
-
-        def W(f, g, engine="s", ts=(0, 1, 2, 3)):
-            gi, off, w, lo = chunks[f]
-            for t in ts:
-                for b in range(w // BLOCK):
-                    col = lo + b * BLOCK
-                    src = r_raw[:, g, t, col : col + BLOCK].bitcast(FP8)
-                    dst = wide[f, g][:, t, b * BLOCK : (b + 1) * BLOCK]
-                    sc = r_sc[:, g, t, col // BLOCK : col // BLOCK + 1]
-                    if engine == "v":
-                        nc.vector.tensor_scalar(out=dst, in0=src, scalar1=sc, scalar2=None, op0=MULT)
-                    else:
-                        nc.scalar.activation(out=dst, in_=src, func=COPY, scale=sc)
-
-        def Mx(f, g, engine="v"):
+        def mix(f, g):
             dst = mixed[f, g][:].rearrange("p (c i) t -> p c t i", i=4)
             src = wide[f, g][:].rearrange("p t (c i) -> p c t i", i=4)
-            if engine == "v":
-                nc.vector.tensor_copy(out=dst, in_=src)
-            else:
-                nc.scalar.copy(out=dst, in_=src)
+            nc.vector.tensor_copy(out=dst, in_=src)
 
-        def Q(f, g):
-            gi, off, w, lo = chunks[f]
+        def quant_r(f, g):
             nc.vector.quantize_mx(
-                out=r_codes[gi][:, g, off : off + w].bitcast(FP8X4),
-                scales=r_planes[gi][:, g, off : off + w],
+                out=r_codes[f, g][:].bitcast(FP8X4),
+                scales=r_planes[f, g][:],
                 in_=mixed[f, g][:].rearrange("p n t -> p (n t)"),
             )
 
-        def KS():
+        def reorder_k_scales():
             nc.vector.tensor_copy(
                 out=k_sc[:].rearrange("p (t m) -> p t m", t=PACK), in_=ks_raw[:].rearrange("p (m t) -> p t m", t=PACK)
             )
 
-        def KW(half):
+        def reorder_k_words(g):
             nc.vector.tensor_copy(
-                out=k_codes[:].bitcast(I32).rearrange("p g (t m) -> p g t m", t=PACK)[:, :, 2 * half : 2 * half + 2, :],
-                in_=k_raw[:].bitcast(I32).rearrange("p g (m t) -> p g t m", t=PACK)[:, :, 2 * half : 2 * half + 2, :],
+                out=k_codes[:, g, :].bitcast(I32).rearrange("p (t m) -> p t m", t=PACK),
+                in_=k_raw[:, g, :].bitcast(I32).rearrange("p (m t) -> p t m", t=PACK),
             )
-
-        def VEC(i):
-            nc.vector.tensor_copy(out=vec[:, i, :], in_=vec_bf[:, i, 0:PACK])
 
         kr = {}
 
-        def K(f):
-            gi, off, w, lo = chunks[f]
-            per = BANK // w
-            for b in range(PACK // per):
-                bank = psum.tile([P, per, w], F32, name="bank")
-                kr[f, b] = bank
-                for i in range(per):
-                    cols = slice((b * per + i) * P, (b * per + i + 1) * P)
-                    for g in range(2):
-                        nc.tensor.matmul_mx(
-                            out=bank[:, i, :],
-                            lhsT=k_codes[:, g, cols].bitcast(FP8X4),
-                            lhsT_scale=k_sc[4 * g : P, cols],
-                            rhs=r_codes[gi][:, g, off : off + w].bitcast(FP8X4),
-                            rhs_scale=r_planes[gi][:, g, off : off + w],
-                            start=(g == 0),
-                            stop=(g == 1),
-                        )
+        def gain(f, groups=(0, 1)):
+            for g in groups:
+                for t in range(PACK):
+                    if g == 0 and t % 2 == 0:
+                        kr[f, t // 2] = k_psum.tile([P, 2, W], F32, name="k_bank")
+                    cols = slice(t * P, (t + 1) * P)
+                    nc.tensor.matmul_mx(
+                        out=kr[f, t // 2][:, t % 2, :],
+                        lhsT=k_codes[:, g, cols].bitcast(FP8X4),
+                        lhsT_scale=k_sc[4 * g : P, cols],
+                        rhs=r_codes[f, g][:].bitcast(FP8X4),
+                        rhs_scale=r_planes[f, g][:],
+                        start=(g == 0 and t % 2 == 0),
+                        stop=(g == 1 and t % 2 == 1),
+                    )
 
-        def U(f):
-            gi, off, w, lo = chunks[f]
-            per = BANK // w
+        def error(f):
             for t in range(PACK):
                 nc.vector.scalar_tensor_tensor(
-                    out=u32[gi][:, t, off : off + w],
-                    in0=v_sb[:, t, lo : lo + w],
-                    scalar=vec[:, 0, t : t + 1],
-                    in1=kr[f, t // per][:, t % per, :],
+                    out=u32[f][:, t, :],
+                    in0=v_sb[:, t, f * W : (f + 1) * W],
+                    scalar=finv_bf[:, t : t + 1],
+                    in1=kr[f, t // 2][:, t % 2, :],
                     op0=MULT,
                     op1=SUB,
                 )
 
-        def J(f):
-            gi, off, w, lo = chunks[f]
-            nc.vector.tensor_copy(out=u_mixed[f][:], in_=u32[gi][:, :, off : off + w].rearrange("p t n -> p n t"))
+        def mix_u(f):
+            nc.vector.tensor_copy(out=u_mixed[f][:], in_=u32[f][:].rearrange("p t n -> p n t"))
 
-        def Pq(f):
-            gi, off, w, lo = chunks[f]
+        def quant_u(f):
             nc.vector.quantize_mx(
-                out=u_codes[gi][:, off : off + w].bitcast(FP8X4),
-                scales=u_planes[gi][:, off : off + w],
+                out=u_codes[f][:].bitcast(FP8X4),
+                scales=u_planes[f][:],
                 in_=u_mixed[f][:].rearrange("p n t -> p (n t)"),
             )
 
-        def E(f, ts, engine):
-            gi, off, w, lo = chunks[f]
+        def disturb(f, engine, ts=range(PACK)):
             for t in ts:
-                src, dst = u32[gi][:, t, off : off + w], eps[gi][:, t, off : off + w]
+                src, dst = u32[f][:, t, :], eps[f][:, t, :]
                 if engine == "v":
-                    nc.vector.tensor_scalar(out=dst, in0=src, scalar1=vec[:, 1, t : t + 1], scalar2=None, op0=MULT)
+                    nc.vector.tensor_scalar(out=dst, in0=src, scalar1=h_f32[:, t : t + 1], scalar2=None, op0=MULT)
                 else:
-                    nc.scalar.activation(out=dst, in_=src, func=COPY, scale=vec[:, 1, t : t + 1])
+                    nc.scalar.activation(out=dst, in_=src, func=COPY, scale=h_f32[:, t : t + 1])
 
-        def store_eps(gi):
-            nc.sync.dma_start(
-                out=eps_view[:, :, group_start[gi] : group_start[gi] + group_width[gi]], in_=eps[gi][:]
-            )
+        def store_eps(f):
+            nc.sync.dma_start(out=eps_view[:, :, f * W : (f + 1) * W], in_=eps[f][:])
 
         acc = {}
 
-        def open_bank(gi, b):
-            acc[gi, b] = psum.tile([P, SLICES[gi], group_width[gi]], F32, name="bank")
+        def transition(f, banks, groups=(0, 1)):
+            for g in groups:
+                for b in banks:
+                    if g == 0:
+                        acc[f, b] = o_psum.tile([P, 2, W], F32, name="o_bank")
+                    for i in range(2):
+                        cols = slice((2 * b + i) * P, (2 * b + i + 1) * P)
+                        nc.tensor.matmul_mx(
+                            out=acc[f, b][:, i, :],
+                            lhsT=t_codes[g][:, cols].bitcast(FP8X4),
+                            lhsT_scale=t_sc[4 * g : P, cols],
+                            rhs=r_codes[f, g][:].bitcast(FP8X4),
+                            rhs_scale=r_planes[f, g][:],
+                            start=(g == 0 and i == 0),
+                            stop=False,
+                        )
 
-        def transition(gi, b, i):
-            s = b * SLICES[gi] + i
-            cols = slice(s * P, (s + 1) * P)
-            for g in range(2):
-                nc.tensor.matmul_mx(
-                    out=acc[gi, b][:, i, :],
-                    lhsT=t_codes[:, g, cols].bitcast(FP8X4),
-                    lhsT_scale=t_sc[4 * g : P, cols],
-                    rhs=r_codes[gi][:, g, :].bitcast(FP8X4),
-                    rhs_scale=r_planes[gi][:, g, :],
-                    start=(g == 0),
-                    stop=False,
-                )
+        def observe(f, banks):
+            for b in banks:
+                for i in range(2):
+                    cols = slice((2 * b + i) * P, (2 * b + i + 1) * P)
+                    nc.tensor.matmul_mx(
+                        out=acc[f, b][:, i, :],
+                        lhsT=z_codes[:, cols].bitcast(FP8X4),
+                        lhsT_scale=z_sc[:, cols],
+                        rhs=u_codes[f][:].bitcast(FP8X4),
+                        rhs_scale=u_planes[f][:],
+                        start=False,
+                        stop=(i == 1),
+                    )
 
-        def observe(gi, b, i):
-            s = b * SLICES[gi] + i
-            cols = slice(s * P, (s + 1) * P)
-            nc.tensor.matmul_mx(
-                out=acc[gi, b][:, i, :],
-                lhsT=z_codes[:, cols].bitcast(FP8X4),
-                lhsT_scale=z_sc[:, cols],
-                rhs=u_codes[gi][:].bitcast(FP8X4),
-                rhs_scale=u_planes[gi][:],
-                start=False,
-                stop=True,
+        def empty(f, b, engine):
+            dst = res[f][:, 2 * b : 2 * b + 2, :]
+            if engine == "v":
+                nc.vector.tensor_copy(out=dst, in_=acc[f, b][:])
+            else:
+                nc.scalar.copy(out=dst, in_=acc[f, b][:])
+
+        def store(f, lo, hi):
+            nc.sync.dma_start(
+                out=prev_view[:, 2 * lo : 2 * hi, f * W : (f + 1) * W], in_=res[f][:, 2 * lo : 2 * hi, :]
             )
 
-        def T(gi, banks):
-            for b in banks:
-                open_bank(gi, b)
-                transition(gi, b, 0)
-
-        def O(gi, banks, engines):
-            for b, engine in zip(banks, engines):
-                if (gi, b) not in acc:
-                    open_bank(gi, b)
-                    transition(gi, b, 0)
-                observe(gi, b, 0)
-                for i in range(1, SLICES[gi]):
-                    transition(gi, b, i)
-                    observe(gi, b, i)
-                per, w, lo = SLICES[gi], group_width[gi], group_start[gi]
-                res = keep.tile([P, per, w], F32, name="res%d_%d" % (gi, b), align_bytes=256)
-                if engine == "v":
-                    nc.vector.tensor_copy(out=res[:], in_=acc[gi, b][:])
-                else:
-                    nc.scalar.copy(out=res[:], in_=acc[gi, b][:])
-                nc.sync.dma_start(out=prev_view[:, b * per : (b + 1) * per, lo : lo + w], in_=res[:])
-
-        def WARM(n):
-            bank = psum.tile([P, BANK], F32, name="bank")
-            src = wide[0, 0]
+        def warm_up(src, n):
+            bank = o_psum.tile([P, 2, W], F32, name="o_bank")
             for i in range(n):
                 nc.tensor.matmul(
-                    bank[:],
+                    bank[:].rearrange("p i n -> p (i n)"),
                     lhsT=src[:, 0, 0:P],
                     rhs=src[:, 0:2, :].rearrange("p t n -> p (t n)"),
                     start=True,
                     stop=True,
                 )
 
-        W(0, 0, "v", (0, 1))
-        W(0, 0, "s", (2, 3))
-        WARM(8)
-        W(1, 0, "s", (0, 1))
-        Mx(0, 0)
-        KS()
-        W(0, 1, "s", (0, 1))
-        W(0, 1, "v", (2, 3))
-        Q(0, 0)
-        Mx(0, 1)
-        W(1, 0, "s", (2, 3))
-        W(1, 1)
-        W(2, 0)
-        W(2, 1)
-        KW(0)
-        Q(0, 1)
-        KW(1)
-        K(0)
-        T(0, range(4))
-        VEC(0)
-        Mx(1, 0)
-        Mx(1, 1)
-        Q(1, 0)
-        Q(1, 1)
-        K(1)
-        U(0)
-        VEC(1)
-        W(3, 0)
-        J(0)
-        E(0, (0, 1, 2, 3), "s")
+        spare = sbuf("spare", [P, 2], F32)
+        nc.vector.memset(spare[:, 0:1], 0.0)
+        nc.scalar.activation(out=spare[:, 1:2], in_=spare[:, 0:1], func=COPY)
+
+        for plane in (ks_raw, t_sc, z_sc):
+            nc.vector.memset(plane[:].bitcast(U32), 0)
+        nc.sync.dma_start(out=r_sc[:], in_=r_scale.rearrange("(g p t) j -> p g t j", p=P, t=PACK))
+        nc.sync.dma_start(out=r_raw[0][:], in_=r_view[:, 0])
+        nc.sync.dma_start(out=r_raw[1][:], in_=r_view[:, 1])
+        load_planes(ks_raw, k_scales, 2)
+        nc.sync.dma_start(out=k_raw[:].bitcast(I32), in_=k_dram)
+        nc.sync.dma_start(out=t_codes[0][:].bitcast(I32), in_=t_dram[0])
+        load_planes(t_sc, t_scales, 2)
+        nc.sync.dma_start(out=finv_bf[:], in_=finv.rearrange("(p t) -> p t", t=PACK))
+        load_v(0, W)
+        nc.sync.dma_start(out=t_codes[1][:].bitcast(I32), in_=t_dram[1])
+        nc.sync.dma_start(out=h_bf[:], in_=h.rearrange("(p t) -> p t", t=PACK))
+        load_planes(z_sc, z_scales, 1)
+        nc.sync.dma_start(out=z_codes[:].bitcast(I32), in_=z_dram)
+        load_v(W, 2 * W)
+        load_v(2 * W, M)
+
+        widen(0, 0, "v", range(0, 5))
+        widen(0, 0, "s", range(5, 8))
+        widen(1, 0, "s", range(0, 4))
+        mix(0, 0)
+        widen(0, 1, "s", range(4, 8))
+        widen(0, 1, "v", range(0, 4))
+        warm_up(wide[0, 1], 3)
+        quant_r(0, 0)
+        mix(0, 1)
+        widen(1, 0, "s", range(4, 8))
+        widen(1, 1, "s", range(8))
+        widen(2, 0, "s", range(8))
+        widen(2, 1, "s", range(8))
+        reorder_k_scales()
+        reorder_k_words(0)
+        quant_r(0, 1)
+        reorder_k_words(1)
+        gain(0)
+        transition(0, range(4), (0,))
+        mix(1, 0)
+        mix(1, 1)
+        quant_r(1, 0)
+        transition(1, range(2), (0,))
+        transition(0, range(4), (1,))
+        error(0)
+        nc.scalar.copy(out=h_f32[:], in_=h_bf[:])
+        disturb(0, "s")
         store_eps(0)
-        W(3, 1)
-        T(1, range(2))
-        Pq(0)
-        O(0, range(4), "ssss")
-        Mx(2, 0)
-        Mx(2, 1)
-        U(1)
-        Q(2, 0)
-        Q(2, 1)
-        K(2)
-        J(1)
-        E(1, (0, 1, 2, 3), "s")
+        quant_r(1, 1)
+        mix_u(0)
+        mix(2, 0)
+        quant_u(0)
+        gain(1)
+        observe(0, range(4))
+        transition(1, range(2), (1,))
+        widen(3, 0, "s", range(0, 8))
+        for b in range(4):
+            empty(0, b, "s")
+            store(0, b, b + 1)
+        widen(3, 1, "s", range(8))
+        transition(1, range(2, 4))
+        mix(2, 1)
+        error(1)
+        quant_r(2, 0)
+        mix_u(1)
+        quant_r(2, 1)
+        quant_u(1)
+        disturb(1, "v")
         store_eps(1)
-        Pq(1)
-        T(1, range(2, 3))
-        O(1, range(4), "ssss")
-        Mx(3, 0)
-        Mx(3, 1)
-        U(2)
-        Q(3, 0)
-        Q(3, 1)
-        T(2, range(2))
-        K(3)
-        J(2)
-        E(2, (0, 1, 2, 3), "s")
+        gain(2)
+        observe(1, range(4))
+        transition(2, range(2))
+        for b in range(4):
+            empty(1, b, "s")
+            store(1, b, b + 1)
+        transition(2, range(2, 4))
+        mix(3, 0)
+        mix(3, 1)
+        error(2)
+        disturb(2, "s")
         store_eps(2)
-        Pq(2)
-        O(2, range(4), "ssss")
-        U(3)
-        J(3)
-        Pq(3)
-        E(3, (0, 1), "s")
-        E(3, (2, 3), "v")
+        quant_r(3, 0)
+        mix_u(2)
+        quant_r(3, 1)
+        quant_u(2)
+        gain(3)
+        observe(2, range(4))
+        transition(3, range(2))
+        for b in range(4):
+            empty(2, b, "s")
+            store(2, b, b + 1)
+        error(3)
+        mix_u(3)
+        disturb(3, "v", range(0, 2))
+        quant_u(3)
+        disturb(3, "v", range(2, 4))
         store_eps(3)
-        O(3, range(8), "vsvsvsvs")
+        transition(3, range(2, 3))
+        observe(3, range(3))
+        transition(3, range(3, 4))
+        observe(3, range(3, 4))
+        for b in range(4):
+            empty(3, b, "v" if b % 2 else "s")
+            store(3, b, b + 1)

@@ -75,9 +75,9 @@ def tile_durbinkoopmandisturbancesmootherstep_d1p_kernel(
         t_dram = t_words.rearrange("g p n t -> g p (n t)").bitcast(I32)
         z_dram = z_words[0].rearrange("p n t -> p (n t)").bitcast(I32)
 
-        def load_planes(plane, scales, groups):
+        def load_planes(queue, plane, scales, groups):
             for q in range(4):
-                nc.sync.dma_start(
+                queue.dma_start(
                     out=plane[32 * q : 32 * q + 4 * groups, :].bitcast(I32),
                     in_=scales[:, 4 * q : 4 * q + 4, :].bitcast(I32),
                 )
@@ -116,8 +116,8 @@ def tile_durbinkoopmandisturbancesmootherstep_d1p_kernel(
 
         def reorder_k_words(g):
             nc.vector.tensor_copy(
-                out=k_codes[:, g, :].bitcast(I32).rearrange("p (t m) -> p t m", t=PACK),
-                in_=k_raw[:, g, :].bitcast(I32).rearrange("p (m t) -> p t m", t=PACK),
+                out=k_codes[:, g, :].bitcast(I32).rearrange("p (t c i) -> p c t i", t=PACK, i=4),
+                in_=k_raw[:, g, :].bitcast(I32).rearrange("p (c i t) -> p c t i", t=PACK, i=4),
             )
 
         kr = {}
@@ -150,7 +150,9 @@ def tile_durbinkoopmandisturbancesmootherstep_d1p_kernel(
                 )
 
         def mix_u(f):
-            nc.vector.tensor_copy(out=u_mixed[f][:], in_=u32[f][:].rearrange("p t n -> p n t"))
+            dst = u_mixed[f][:].rearrange("p (c i) t -> p c t i", i=4)
+            src = u32[f][:].rearrange("p t (c i) -> p c t i", i=4)
+            nc.vector.tensor_copy(out=dst, in_=src)
 
         def quant_u(f):
             nc.vector.quantize_mx(
@@ -235,15 +237,15 @@ def tile_durbinkoopmandisturbancesmootherstep_d1p_kernel(
         nc.sync.dma_start(out=r_sc[:], in_=r_scale.rearrange("(g p t) j -> p g t j", p=P, t=PACK))
         nc.sync.dma_start(out=r_raw[0][:], in_=r_view[:, 0])
         nc.sync.dma_start(out=r_raw[1][:], in_=r_view[:, 1])
-        load_planes(ks_raw, k_scales, 2)
+        load_planes(nc.sync, ks_raw, k_scales, 2)
         nc.sync.dma_start(out=k_raw[:].bitcast(I32), in_=k_dram)
         nc.sync.dma_start(out=t_codes[0][:].bitcast(I32), in_=t_dram[0])
-        load_planes(t_sc, t_scales, 2)
+        load_planes(nc.sync, t_sc, t_scales, 2)
         nc.sync.dma_start(out=finv_bf[:], in_=finv.rearrange("(p t) -> p t", t=PACK))
         load_v(0, W)
-        nc.sync.dma_start(out=t_codes[1][:].bitcast(I32), in_=t_dram[1])
         nc.sync.dma_start(out=h_bf[:], in_=h.rearrange("(p t) -> p t", t=PACK))
-        load_planes(z_sc, z_scales, 1)
+        nc.sync.dma_start(out=t_codes[1][:].bitcast(I32), in_=t_dram[1])
+        load_planes(nc.sync, z_sc, z_scales, 1)
         nc.sync.dma_start(out=z_codes[:].bitcast(I32), in_=z_dram)
         load_v(W, 2 * W)
         load_v(2 * W, M)
@@ -260,75 +262,54 @@ def tile_durbinkoopmandisturbancesmootherstep_d1p_kernel(
         widen(1, 0, "s", range(4, 8))
         widen(1, 1, "s", range(8))
         widen(2, 0, "s", range(8))
+        nc.scalar.copy(out=h_f32[:], in_=h_bf[:])
         widen(2, 1, "s", range(8))
         reorder_k_scales()
         reorder_k_words(0)
         quant_r(0, 1)
         reorder_k_words(1)
         gain(0)
-        transition(0, range(4), (0,))
+        transition(0, range(4))
         mix(1, 0)
-        mix(1, 1)
-        quant_r(1, 0)
-        transition(1, range(2), (0,))
-        transition(0, range(4), (1,))
-        error(0)
-        nc.scalar.copy(out=h_f32[:], in_=h_bf[:])
-        disturb(0, "s")
-        store_eps(0)
-        quant_r(1, 1)
-        mix_u(0)
-        mix(2, 0)
-        quant_u(0)
-        gain(1)
-        observe(0, range(4))
-        transition(1, range(2), (1,))
-        widen(3, 0, "s", range(0, 8))
-        for b in range(4):
-            empty(0, b, "s")
-            store(0, b, b + 1)
-        widen(3, 1, "s", range(8))
-        transition(1, range(2, 4))
-        mix(2, 1)
-        error(1)
-        quant_r(2, 0)
-        mix_u(1)
-        quant_r(2, 1)
-        quant_u(1)
-        disturb(1, "v")
-        store_eps(1)
-        gain(2)
-        observe(1, range(4))
-        transition(2, range(2))
-        for b in range(4):
-            empty(1, b, "s")
-            store(1, b, b + 1)
-        transition(2, range(2, 4))
-        mix(3, 0)
-        mix(3, 1)
-        error(2)
-        disturb(2, "s")
-        store_eps(2)
-        quant_r(3, 0)
-        mix_u(2)
-        quant_r(3, 1)
-        quant_u(2)
-        gain(3)
-        observe(2, range(4))
-        transition(3, range(2))
-        for b in range(4):
-            empty(2, b, "s")
-            store(2, b, b + 1)
-        error(3)
-        mix_u(3)
-        disturb(3, "v", range(0, 2))
-        quant_u(3)
-        disturb(3, "v", range(2, 4))
-        store_eps(3)
-        transition(3, range(2, 3))
-        observe(3, range(3))
-        transition(3, range(3, 4))
-        observe(3, range(3, 4))
-        for b in range(4):
-            empty(3, b, "v" if b % 2 else "s")
-            store(3, b, b + 1)
+
+        for f in range(CHUNKS):
+            more = f + 1 < CHUNKS
+            error(f)
+            if more:
+                quant_r(f + 1, 0)
+                if f < 2 or 1:
+                    gain(f + 1, (0,))
+                disturb(f, "s")
+            else:
+                disturb(f, "v", range(2))
+            mix_u(f)
+            if f == 0:
+                transition(1, range(2), (0,))
+                widen(3, 0, "s", range(8))
+            if f == 1:
+                widen(3, 1, "s", range(2, 6))
+            if more:
+                mix(f + 1, 1)
+            else:
+                disturb(f, "v", range(2, 4))
+            store_eps(f)
+            quant_u(f)
+            observe(f, range(1))
+            if more:
+                quant_r(f + 1, 1)
+                gain(f + 1, (1,) if f < 2 or 1 else (0, 1))
+            if f + 2 < CHUNKS:
+                mix(f + 2, 0)
+            if f == 0:
+                widen(3, 1, "v", range(6, 8))
+            observe(f, range(1, 4))
+            for b in range(4):
+                empty(f, b, "s" if more or b % 2 == 0 else "v")
+                store(f, b, b + 1)
+                if f == 0 and b == 0:
+                    widen(3, 1, "s", range(0, 2))
+            if f == 0:
+                transition(1, range(2), (1,))
+            if more:
+                for b in range(2 if f == 0 else 0, 4):
+                    transition(f + 1, (b,))

@@ -41,7 +41,10 @@ def tile_durbinkoopmandisturbancesmootherstep_d1p_kernel(
         def sbuf(name, shape, dtype):
             return keep.tile(shape, dtype, name=name, align_bytes=256)
 
-        r_raw = [sbuf("r_raw%d" % g, [P, PACK, M], U8) for g in range(2)]
+        r_raw = {}
+        for half in range(2):
+            for g in range(2):
+                r_raw[half, g] = sbuf("r_raw%d_%d" % (half, g), [P, PACK, M // 2], U8)
         r_sc = sbuf("r_sc", [P, 2, PACK, M // BLOCK], F32)
         v_sb = sbuf("v_sb", [P, PACK, M], BF16)
         finv_bf = sbuf("finv_bf", [P, PACK], BF16)
@@ -53,7 +56,7 @@ def tile_durbinkoopmandisturbancesmootherstep_d1p_kernel(
         k_sc = sbuf("k_sc", [P, P_OBS], U8)
         t_codes = [sbuf("t_codes%d" % g, [P, S], U32) for g in range(2)]
         z_codes = sbuf("z_codes", [P, S], U32)
-        t_sc = sbuf("t_sc", [P, S], U8)
+        t_sc = sbuf("t_sc", [P, 2, S], U8)
         z_sc = sbuf("z_sc", [P, S], U8)
 
         wide, mixed, r_codes, r_planes = {}, {}, {}, {}
@@ -66,7 +69,8 @@ def tile_durbinkoopmandisturbancesmootherstep_d1p_kernel(
             eps[f] = sbuf("eps%d" % f, [P, PACK, W], F32)
             res[f] = sbuf("res%d" % f, [P, S // P, W], F32)
             for g in range(2):
-                wide[f, g] = sbuf("wide%d_%d" % (f, g), [P, PACK, W], BF16)
+                if f > 0:
+                    wide[f, g] = sbuf("wide%d_%d" % (f, g), [P, PACK, W], BF16)
                 mixed[f, g] = sbuf("mixed%d_%d" % (f, g), [P, W, PACK], BF16)
                 r_codes[f, g] = sbuf("r_codes%d_%d" % (f, g), [P, W], U32)
                 r_planes[f, g] = sbuf("r_planes%d_%d" % (f, g), [P, W], U8)
@@ -82,6 +86,16 @@ def tile_durbinkoopmandisturbancesmootherstep_d1p_kernel(
                     in_=scales[:, 4 * q : 4 * q + 4, :].bitcast(I32),
                 )
 
+        def load_t_planes():
+            for q in range(4):
+                nc.sync.dma_start(
+                    out=t_sc[32 * q + 4 : 32 * q + 8, :, :].bitcast(I32),
+                    in_=t_scales[:, 4 * q : 4 * q + 4, :].rearrange("g r n -> r g n").bitcast(I32),
+                )
+
+        def load_r(half, g):
+            nc.sync.dma_start(out=r_raw[half, g][:], in_=r_view[:, g, :, half * M // 2 : (half + 1) * M // 2])
+
         def load_v(lo, hi):
             nc.sync.dma_start(out=v_sb[:, :, lo:hi], in_=v_view[:, :, lo:hi])
 
@@ -89,7 +103,8 @@ def tile_durbinkoopmandisturbancesmootherstep_d1p_kernel(
             for i in blocks:
                 t, b = divmod(i, W // BLOCK)
                 col = f * W + b * BLOCK
-                src = r_raw[g][:, t, col : col + BLOCK].bitcast(FP8)
+                at = col % (M // 2)
+                src = r_raw[f // 2, g][:, t, at : at + BLOCK].bitcast(FP8)
                 dst = wide[f, g][:, t, b * BLOCK : (b + 1) * BLOCK]
                 sc = r_sc[:, g, t, col // BLOCK : col // BLOCK + 1]
                 if engine == "v":
@@ -97,10 +112,35 @@ def tile_durbinkoopmandisturbancesmootherstep_d1p_kernel(
                 else:
                     nc.scalar.activation(out=dst, in_=src, func=COPY, scale=sc)
 
-        def mix(f, g):
+        paired = {}
+
+        def widen_pairs(f, g, blocks=range(8)):
+            if (f, g) not in paired:
+                paired[f, g] = sbuf("paired%d_%d" % (f, g), [P, 2, W, 2], BF16)
+            for i in blocks:
+                t, b = divmod(i, W // BLOCK)
+                col = f * W + b * BLOCK
+                at = col % (M // 2)
+                nc.vector.tensor_scalar(
+                    out=paired[f, g][:, t // 2, b * BLOCK : (b + 1) * BLOCK, t % 2],
+                    in0=r_raw[f // 2, g][:, t, at : at + BLOCK].bitcast(FP8),
+                    scalar1=r_sc[:, g, t, col // BLOCK : col // BLOCK + 1],
+                    scalar2=None,
+                    op0=MULT,
+                )
+
+        def mix_pairs(f, g):
+            dst = mixed[f, g][:].rearrange("p n t -> p (n t)").bitcast(U32).rearrange("p (n u) -> p n u", u=2)
+            src = paired[f, g][:].rearrange("p u n e -> p u (n e)").bitcast(U32).rearrange("p u n -> p n u")
+            nc.scalar.copy(out=dst, in_=src)
+
+        def mix(f, g, engine="v"):
             dst = mixed[f, g][:].rearrange("p (c i) t -> p c t i", i=4)
             src = wide[f, g][:].rearrange("p t (c i) -> p c t i", i=4)
-            nc.vector.tensor_copy(out=dst, in_=src)
+            if engine == "v":
+                nc.vector.tensor_copy(out=dst, in_=src)
+            else:
+                nc.scalar.copy(out=dst, in_=src)
 
         def quant_r(f, g):
             nc.vector.quantize_mx(
@@ -149,10 +189,13 @@ def tile_durbinkoopmandisturbancesmootherstep_d1p_kernel(
                     op1=SUB,
                 )
 
-        def mix_u(f):
+        def mix_u(f, engine="v"):
             dst = u_mixed[f][:].rearrange("p (c i) t -> p c t i", i=4)
             src = u32[f][:].rearrange("p t (c i) -> p c t i", i=4)
-            nc.vector.tensor_copy(out=dst, in_=src)
+            if engine == "v":
+                nc.vector.tensor_copy(out=dst, in_=src)
+            else:
+                nc.scalar.copy(out=dst, in_=src)
 
         def quant_u(f):
             nc.vector.quantize_mx(
@@ -173,18 +216,21 @@ def tile_durbinkoopmandisturbancesmootherstep_d1p_kernel(
             nc.sync.dma_start(out=eps_view[:, :, f * W : (f + 1) * W], in_=eps[f][:])
 
         acc = {}
+        pairs = [(0, 1), (2, 3), (4, 5), (6, 7)]
+        groups_of = {f: pairs for f in range(CHUNKS)}
+        groups_of[CHUNKS - 1] = pairs[:3] + [(6,), (7,)]
 
         def transition(f, banks, groups=(0, 1)):
             for g in groups:
                 for b in banks:
                     if g == 0:
-                        acc[f, b] = o_psum.tile([P, 2, W], F32, name="o_bank")
-                    for i in range(2):
-                        cols = slice((2 * b + i) * P, (2 * b + i + 1) * P)
+                        acc[f, b] = o_psum.tile([P, len(groups_of[f][b]), W], F32, name="o_bank")
+                    for i, s in enumerate(groups_of[f][b]):
+                        cols = slice(s * P, (s + 1) * P)
                         nc.tensor.matmul_mx(
                             out=acc[f, b][:, i, :],
                             lhsT=t_codes[g][:, cols].bitcast(FP8X4),
-                            lhsT_scale=t_sc[4 * g : P, cols],
+                            lhsT_scale=t_sc[4:P, g, cols],
                             rhs=r_codes[f, g][:].bitcast(FP8X4),
                             rhs_scale=r_planes[f, g][:],
                             start=(g == 0 and i == 0),
@@ -193,8 +239,8 @@ def tile_durbinkoopmandisturbancesmootherstep_d1p_kernel(
 
         def observe(f, banks):
             for b in banks:
-                for i in range(2):
-                    cols = slice((2 * b + i) * P, (2 * b + i + 1) * P)
+                for i, s in enumerate(groups_of[f][b]):
+                    cols = slice(s * P, (s + 1) * P)
                     nc.tensor.matmul_mx(
                         out=acc[f, b][:, i, :],
                         lhsT=z_codes[:, cols].bitcast(FP8X4),
@@ -202,28 +248,28 @@ def tile_durbinkoopmandisturbancesmootherstep_d1p_kernel(
                         rhs=u_codes[f][:].bitcast(FP8X4),
                         rhs_scale=u_planes[f][:],
                         start=False,
-                        stop=(i == 1),
+                        stop=(i == len(groups_of[f][b]) - 1),
                     )
 
         def empty(f, b, engine):
-            dst = res[f][:, 2 * b : 2 * b + 2, :]
+            dst = res[f][:, groups_of[f][b][0] : groups_of[f][b][-1] + 1, :]
             if engine == "v":
                 nc.vector.tensor_copy(out=dst, in_=acc[f, b][:])
             else:
                 nc.scalar.copy(out=dst, in_=acc[f, b][:])
 
         def store(f, lo, hi):
-            nc.sync.dma_start(
-                out=prev_view[:, 2 * lo : 2 * hi, f * W : (f + 1) * W], in_=res[f][:, 2 * lo : 2 * hi, :]
-            )
+            rows = slice(groups_of[f][lo][0], groups_of[f][hi - 1][-1] + 1)
+            nc.sync.dma_start(out=prev_view[:, rows, f * W : (f + 1) * W], in_=res[f][:, rows, :])
 
         def warm_up(src, n):
             bank = o_psum.tile([P, 2, W], F32, name="o_bank")
+            src = src[:, 1].rearrange("p n e -> p (n e)")
             for i in range(n):
                 nc.tensor.matmul(
                     bank[:].rearrange("p i n -> p (i n)"),
-                    lhsT=src[:, 0, 0:P],
-                    rhs=src[:, 0:2, :].rearrange("p t n -> p (t n)"),
+                    lhsT=src[:, 0:P],
+                    rhs=src,
                     start=True,
                     stop=True,
                 )
@@ -235,81 +281,117 @@ def tile_durbinkoopmandisturbancesmootherstep_d1p_kernel(
         for plane in (ks_raw, t_sc, z_sc):
             nc.vector.memset(plane[:].bitcast(U32), 0)
         nc.sync.dma_start(out=r_sc[:], in_=r_scale.rearrange("(g p t) j -> p g t j", p=P, t=PACK))
-        nc.sync.dma_start(out=r_raw[0][:], in_=r_view[:, 0])
-        nc.sync.dma_start(out=r_raw[1][:], in_=r_view[:, 1])
+        load_r(0, 0)
+        load_r(0, 1)
         load_planes(nc.sync, ks_raw, k_scales, 2)
         nc.sync.dma_start(out=k_raw[:].bitcast(I32), in_=k_dram)
-        nc.sync.dma_start(out=t_codes[0][:].bitcast(I32), in_=t_dram[0])
-        load_planes(nc.sync, t_sc, t_scales, 2)
+        load_r(1, 0)
         nc.sync.dma_start(out=finv_bf[:], in_=finv.rearrange("(p t) -> p t", t=PACK))
-        load_v(0, W)
         nc.sync.dma_start(out=h_bf[:], in_=h.rearrange("(p t) -> p t", t=PACK))
+        nc.sync.dma_start(out=t_codes[0][:].bitcast(I32), in_=t_dram[0])
+        load_t_planes()
+        load_v(0, W)
         nc.sync.dma_start(out=t_codes[1][:].bitcast(I32), in_=t_dram[1])
+        load_r(1, 1)
         load_planes(nc.sync, z_sc, z_scales, 1)
         nc.sync.dma_start(out=z_codes[:].bitcast(I32), in_=z_dram)
         load_v(W, 2 * W)
         load_v(2 * W, M)
 
-        widen(0, 0, "v", range(0, 5))
-        widen(0, 0, "s", range(5, 8))
-        widen(1, 0, "s", range(0, 4))
-        mix(0, 0)
-        widen(0, 1, "s", range(4, 8))
-        widen(0, 1, "v", range(0, 4))
-        warm_up(wide[0, 1], 3)
-        quant_r(0, 0)
-        mix(0, 1)
-        widen(1, 0, "s", range(4, 8))
-        widen(1, 1, "s", range(8))
+        widen_pairs(0, 0)
+        warm_up(paired[0, 0], 2)
+        widen(1, 0, "s", range(8))
+        mix_pairs(0, 0)
+        widen_pairs(0, 1)
+        warm_up(paired[0, 1], 2)
+        widen(1, 1, "s", range(2))
+        mix_pairs(0, 1)
+        widen(1, 1, "s", range(2, 8))
         widen(2, 0, "s", range(8))
-        nc.scalar.copy(out=h_f32[:], in_=h_bf[:])
-        widen(2, 1, "s", range(8))
+        widen(3, 0, "s", range(8))
         reorder_k_scales()
+        quant_r(0, 0)
         reorder_k_words(0)
-        quant_r(0, 1)
         reorder_k_words(1)
+        quant_r(0, 1)
         gain(0)
-        transition(0, range(4))
+        transition(0, range(4), (0,))
         mix(1, 0)
-
-        for f in range(CHUNKS):
-            more = f + 1 < CHUNKS
-            error(f)
-            if more:
-                quant_r(f + 1, 0)
-                if f < 2 or 1:
-                    gain(f + 1, (0,))
-                disturb(f, "s")
-            else:
-                disturb(f, "v", range(2))
-            mix_u(f)
-            if f == 0:
-                transition(1, range(2), (0,))
-                widen(3, 0, "s", range(8))
-            if f == 1:
-                widen(3, 1, "s", range(2, 6))
-            if more:
-                mix(f + 1, 1)
-            else:
-                disturb(f, "v", range(2, 4))
-            store_eps(f)
-            quant_u(f)
-            observe(f, range(1))
-            if more:
-                quant_r(f + 1, 1)
-                gain(f + 1, (1,) if f < 2 or 1 else (0, 1))
-            if f + 2 < CHUNKS:
-                mix(f + 2, 0)
-            if f == 0:
-                widen(3, 1, "v", range(6, 8))
-            observe(f, range(1, 4))
-            for b in range(4):
-                empty(f, b, "s" if more or b % 2 == 0 else "v")
-                store(f, b, b + 1)
-                if f == 0 and b == 0:
-                    widen(3, 1, "s", range(0, 2))
-            if f == 0:
-                transition(1, range(2), (1,))
-            if more:
-                for b in range(2 if f == 0 else 0, 4):
-                    transition(f + 1, (b,))
+        mix(1, 1)
+        quant_r(1, 0)
+        transition(1, range(2), (0,))
+        nc.scalar.copy(out=h_f32[:], in_=h_bf[:])
+        error(0)
+        transition(0, range(4), (1,))
+        gain(1, (0,))
+        disturb(0, "s")
+        widen(2, 1, "s", range(8))
+        quant_r(1, 1)
+        mix_u(0)
+        mix(2, 0)
+        store_eps(0)
+        quant_u(0)
+        quant_r(2, 0)
+        gain(1, (1,))
+        observe(0, range(4))
+        mix(3, 0)
+        for b in range(4):
+            empty(0, b, "s")
+            store(0, b, b + 1)
+        transition(1, range(2), (1,))
+        for b in range(2, 4):
+            transition(1, (b,))
+        error(1)
+        gain(2, (0,))
+        transition(2, (0,), (0,))
+        disturb(1, "s")
+        mix(2, 1)
+        mix_u(1)
+        quant_r(2, 1)
+        gain(2, (1,))
+        widen(3, 1, "s", range(5))
+        store_eps(1)
+        quant_u(1)
+        observe(1, range(4))
+        widen(3, 1, "v", range(5, 8))
+        quant_r(3, 0)
+        for b in range(4):
+            empty(1, b, "s")
+            store(1, b, b + 1)
+        transition(2, (0,), (1,))
+        transition(2, (1,))
+        error(2)
+        gain(3, (0,))
+        for b in range(2, 3):
+            transition(2, (b,))
+        disturb(2, "s", range(2))
+        mix(3, 1)
+        mix_u(2)
+        quant_r(3, 1)
+        quant_u(2)
+        disturb(2, "v", range(2, 4))
+        store_eps(2)
+        observe(2, range(1))
+        gain(3, (1,))
+        observe(2, range(1, 3))
+        for b in range(3, 4):
+            transition(2, (b,))
+            observe(2, (b,))
+        for b in range(4):
+            empty(2, b, "s")
+            store(2, b, b + 1)
+        for b in range(3):
+            transition(3, (b,))
+        error(3)
+        disturb(3, "v", range(2))
+        mix_u(3)
+        disturb(3, "v", range(2, 4))
+        store_eps(3)
+        quant_u(3)
+        observe(3, range(3))
+        for b in range(3, 5):
+            transition(3, (b,))
+            observe(3, (b,))
+        for b in range(5):
+            empty(3, b, "vs"[b % 2])
+            store(3, b, b + 1)

@@ -47,9 +47,9 @@ def tile_durbinkoopmandisturbancesmootherstep_d1p_kernel(
                 r_raw[half, g] = sbuf("r_raw%d_%d" % (half, g), [P, PACK, M // 2], U8)
         r_sc = sbuf("r_sc", [P, 2, PACK, M // BLOCK], F32)
         v_sb = sbuf("v_sb", [P, PACK, M], BF16)
-        finv_bf = sbuf("finv_bf", [P, PACK], BF16)
-        h_bf = sbuf("h_bf", [P, PACK], BF16)
-        h_f32 = sbuf("h_f32", [P, PACK], F32)
+        rows = sbuf("rows", [P, P_OBS], BF16)
+        pick = sbuf("pick", [P, 2], BF16)
+        factors = sbuf("factors", [P, PACK, 2], F32)
         k_raw = sbuf("k_raw", [P, 2, P_OBS], U32)
         k_codes = sbuf("k_codes", [P, 2, P_OBS], U32)
         ks_raw = sbuf("ks_raw", [P, P_OBS], U8)
@@ -69,7 +69,7 @@ def tile_durbinkoopmandisturbancesmootherstep_d1p_kernel(
             eps[f] = sbuf("eps%d" % f, [P, PACK, W], F32)
             res[f] = sbuf("res%d" % f, [P, S // P, W], F32)
             for g in range(2):
-                if f > 0:
+                if f > 0 and (f, g) != (2, 1):
                     wide[f, g] = sbuf("wide%d_%d" % (f, g), [P, PACK, W], BF16)
                 mixed[f, g] = sbuf("mixed%d_%d" % (f, g), [P, W, PACK], BF16)
                 r_codes[f, g] = sbuf("r_codes%d_%d" % (f, g), [P, W], U32)
@@ -129,10 +129,13 @@ def tile_durbinkoopmandisturbancesmootherstep_d1p_kernel(
                     op0=MULT,
                 )
 
-        def mix_pairs(f, g):
+        def mix_pairs(f, g, engine="s"):
             dst = mixed[f, g][:].rearrange("p n t -> p (n t)").bitcast(U32).rearrange("p (n u) -> p n u", u=2)
             src = paired[f, g][:].rearrange("p u n e -> p u (n e)").bitcast(U32).rearrange("p u n -> p n u")
-            nc.scalar.copy(out=dst, in_=src)
+            if engine == "v":
+                nc.vector.tensor_copy(out=dst.bitcast(I32), in_=src.bitcast(I32))
+            else:
+                nc.scalar.copy(out=dst, in_=src)
 
         def mix(f, g, engine="v"):
             dst = mixed[f, g][:].rearrange("p (c i) t -> p c t i", i=4)
@@ -183,7 +186,7 @@ def tile_durbinkoopmandisturbancesmootherstep_d1p_kernel(
                 nc.vector.scalar_tensor_tensor(
                     out=u32[f][:, t, :],
                     in0=v_sb[:, t, f * W : (f + 1) * W],
-                    scalar=finv_bf[:, t : t + 1],
+                    scalar=factors[:, t, 0:1],
                     in1=kr[f, t // 2][:, t % 2, :],
                     op0=MULT,
                     op1=SUB,
@@ -208,9 +211,9 @@ def tile_durbinkoopmandisturbancesmootherstep_d1p_kernel(
             for t in ts:
                 src, dst = u32[f][:, t, :], eps[f][:, t, :]
                 if engine == "v":
-                    nc.vector.tensor_scalar(out=dst, in0=src, scalar1=h_f32[:, t : t + 1], scalar2=None, op0=MULT)
+                    nc.vector.tensor_scalar(out=dst, in0=src, scalar1=factors[:, t, 1:2], scalar2=None, op0=MULT)
                 else:
-                    nc.scalar.activation(out=dst, in_=src, func=COPY, scale=h_f32[:, t : t + 1])
+                    nc.scalar.activation(out=dst, in_=src, func=COPY, scale=factors[:, t, 1:2])
 
         def store_eps(f):
             nc.sync.dma_start(out=eps_view[:, :, f * W : (f + 1) * W], in_=eps[f][:])
@@ -264,7 +267,7 @@ def tile_durbinkoopmandisturbancesmootherstep_d1p_kernel(
 
         def warm_up(src, n):
             bank = o_psum.tile([P, 2, W], F32, name="o_bank")
-            src = src[:, 1].rearrange("p n e -> p (n e)")
+            src = src[:, 0].rearrange("p n e -> p (n e)")
             for i in range(n):
                 nc.tensor.matmul(
                     bank[:].rearrange("p i n -> p (i n)"),
@@ -278,6 +281,10 @@ def tile_durbinkoopmandisturbancesmootherstep_d1p_kernel(
         nc.vector.memset(spare[:, 0:1], 0.0)
         nc.scalar.activation(out=spare[:, 1:2], in_=spare[:, 0:1], func=COPY)
 
+        nc.vector.memset(rows[:].bitcast(U32), 0)
+        nc.vector.memset(pick[:], 0.0)
+        nc.vector.memset(pick[0:32, 0:1], 1.0)
+        nc.vector.memset(pick[32:64, 1:2], 1.0)
         for plane in (ks_raw, t_sc, z_sc):
             nc.vector.memset(plane[:].bitcast(U32), 0)
         nc.sync.dma_start(out=r_sc[:], in_=r_scale.rearrange("(g p t) j -> p g t j", p=P, t=PACK))
@@ -286,8 +293,8 @@ def tile_durbinkoopmandisturbancesmootherstep_d1p_kernel(
         load_planes(nc.sync, ks_raw, k_scales, 2)
         nc.sync.dma_start(out=k_raw[:].bitcast(I32), in_=k_dram)
         load_r(1, 0)
-        nc.sync.dma_start(out=finv_bf[:], in_=finv.rearrange("(p t) -> p t", t=PACK))
-        nc.sync.dma_start(out=h_bf[:], in_=h.rearrange("(p t) -> p t", t=PACK))
+        nc.sync.dma_start(out=rows[0:1, :], in_=finv.rearrange("(o n) -> o n", o=1))
+        nc.sync.dma_start(out=rows[32:33, :], in_=h.rearrange("(o n) -> o n", o=1))
         nc.sync.dma_start(out=t_codes[0][:].bitcast(I32), in_=t_dram[0])
         load_t_planes()
         load_v(0, W)
@@ -308,33 +315,37 @@ def tile_durbinkoopmandisturbancesmootherstep_d1p_kernel(
         mix_pairs(0, 1)
         widen(1, 1, "s", range(2, 8))
         widen(2, 0, "s", range(8))
-        widen(3, 0, "s", range(8))
         reorder_k_scales()
         quant_r(0, 0)
         reorder_k_words(0)
         reorder_k_words(1)
         quant_r(0, 1)
         gain(0)
+        spread = o_psum.tile([P, PACK, 2], F32, name="o_bank")
+        for t in range(PACK):
+            nc.tensor.matmul(spread[:, t, :], lhsT=rows[:, t::PACK], rhs=pick[:], start=True, stop=True)
+        nc.scalar.copy(out=factors[:], in_=spread[:])
+        widen(3, 0, "s", range(8))
         transition(0, range(4), (0,))
         mix(1, 0)
         mix(1, 1)
         quant_r(1, 0)
         transition(1, range(2), (0,))
-        nc.scalar.copy(out=h_f32[:], in_=h_bf[:])
+        mix(2, 0, "s")
         error(0)
         transition(0, range(4), (1,))
         gain(1, (0,))
         disturb(0, "s")
-        widen(2, 1, "s", range(8))
+        widen(3, 1, "s", range(2))
         quant_r(1, 1)
         mix_u(0)
-        mix(2, 0)
+        widen_pairs(2, 1, range(4))
         store_eps(0)
         quant_u(0)
+        widen_pairs(2, 1, range(4, 8))
         quant_r(2, 0)
         gain(1, (1,))
         observe(0, range(4))
-        mix(3, 0)
         for b in range(4):
             empty(0, b, "s")
             store(0, b, b + 1)
@@ -343,40 +354,38 @@ def tile_durbinkoopmandisturbancesmootherstep_d1p_kernel(
             transition(1, (b,))
         error(1)
         gain(2, (0,))
-        transition(2, (0,), (0,))
-        disturb(1, "s")
-        mix(2, 1)
+        disturb(1, "s", range(4))
+        mix_pairs(2, 1, "v")
         mix_u(1)
         quant_r(2, 1)
         gain(2, (1,))
-        widen(3, 1, "s", range(5))
+        widen(3, 1, "s", range(2, 5))
         store_eps(1)
         quant_u(1)
         observe(1, range(4))
+        mix(3, 0)
         widen(3, 1, "v", range(5, 8))
-        quant_r(3, 0)
         for b in range(4):
             empty(1, b, "s")
             store(1, b, b + 1)
-        transition(2, (0,), (1,))
+        transition(2, (0,))
         transition(2, (1,))
         error(2)
+        quant_r(3, 0)
+        disturb(2, "v", range(3, 4))
+        transition(2, (2,))
         gain(3, (0,))
-        for b in range(2, 3):
-            transition(2, (b,))
-        disturb(2, "s", range(2))
-        mix(3, 1)
+        disturb(2, "s", range(3))
         mix_u(2)
-        quant_r(3, 1)
+        mix(3, 1)
         quant_u(2)
-        disturb(2, "v", range(2, 4))
+        quant_r(3, 1)
         store_eps(2)
         observe(2, range(1))
         gain(3, (1,))
         observe(2, range(1, 3))
-        for b in range(3, 4):
-            transition(2, (b,))
-            observe(2, (b,))
+        transition(2, (3,))
+        observe(2, (3,))
         for b in range(4):
             empty(2, b, "s")
             store(2, b, b + 1)

@@ -57,7 +57,7 @@ def tile_durbinkoopmandisturbancesmootherstep_d1p_kernel(
         t_codes = [sbuf("t_codes%d" % g, [P, S], U32) for g in range(2)]
         z_codes = sbuf("z_codes", [P, S], U32)
         t_sc = sbuf("t_sc", [P, 2, S], U8)
-        z_sc = sbuf("z_sc", [P, S], U8)
+        z_sc = sbuf("z_sc", [P, S // 4], U8)
 
         wide, mixed, r_codes, r_planes = {}, {}, {}, {}
         u32, u_mixed, u_codes, u_planes, eps, res = {}, {}, {}, {}, {}, {}
@@ -87,10 +87,17 @@ def tile_durbinkoopmandisturbancesmootherstep_d1p_kernel(
                 )
 
         def load_t_planes():
+            for r in range(4):
+                nc.sync.dma_start(
+                    out=t_sc[4 + r : P : 32, :, :].bitcast(I32),
+                    in_=t_scales[:, r:16:4, :].rearrange("g q n -> q g n").bitcast(I32),
+                )
+
+        def load_z_planes():
             for q in range(4):
                 nc.sync.dma_start(
-                    out=t_sc[32 * q + 4 : 32 * q + 8, :, :].bitcast(I32),
-                    in_=t_scales[:, 4 * q : 4 * q + 4, :].rearrange("g r n -> r g n").bitcast(I32),
+                    out=z_sc[32 * q : 32 * q + 16, :].bitcast(I32),
+                    in_=z_scales[0, 4 * q : 4 * q + 4, :].bitcast(I32).rearrange("r (j n) -> j r n", j=4),
                 )
 
         def load_r(half, g):
@@ -247,7 +254,7 @@ def tile_durbinkoopmandisturbancesmootherstep_d1p_kernel(
                     nc.tensor.matmul_mx(
                         out=acc[f, b][:, i, :],
                         lhsT=z_codes[:, cols].bitcast(FP8X4),
-                        lhsT_scale=z_sc[:, cols],
+                        lhsT_scale=z_sc[4 * (s // 2) : P, (s % 2) * P : (s % 2 + 1) * P],
                         rhs=u_codes[f][:].bitcast(FP8X4),
                         rhs_scale=u_planes[f][:],
                         start=False,
@@ -300,7 +307,7 @@ def tile_durbinkoopmandisturbancesmootherstep_d1p_kernel(
         load_v(0, W)
         nc.sync.dma_start(out=t_codes[1][:].bitcast(I32), in_=t_dram[1])
         load_r(1, 1)
-        load_planes(nc.sync, z_sc, z_scales, 1)
+        load_z_planes()
         nc.sync.dma_start(out=z_codes[:].bitcast(I32), in_=z_dram)
         load_v(W, 2 * W)
         load_v(2 * W, M)

@@ -166,8 +166,8 @@ def tile_durbinkoopmandisturbancesmootherstep_d1p_kernel(
 
         def reorder_k_words(g):
             nc.vector.tensor_copy(
-                out=k_codes[:, g, :].bitcast(I32).rearrange("p (t c i) -> p c t i", t=PACK, i=4),
-                in_=k_raw[:, g, :].bitcast(I32).rearrange("p (c i t) -> p c t i", t=PACK, i=4),
+                out=k_codes[:, g, :].bitcast(I32).rearrange("p (t m) -> p m t", t=PACK),
+                in_=k_raw[:, g, :].bitcast(I32).rearrange("p (m t) -> p m t", t=PACK),
             )
 
         kr = {}
@@ -200,8 +200,8 @@ def tile_durbinkoopmandisturbancesmootherstep_d1p_kernel(
                 )
 
         def mix_u(f, engine="v"):
-            dst = u_mixed[f][:].rearrange("p (c i) t -> p c t i", i=4)
-            src = u32[f][:].rearrange("p t (c i) -> p c t i", i=4)
+            dst = u_mixed[f][:].rearrange("p (c i) t -> p c t i", i=2)
+            src = u32[f][:].rearrange("p t (c i) -> p c t i", i=2)
             if engine == "v":
                 nc.vector.tensor_copy(out=dst, in_=src)
             else:

@@ -56,7 +56,7 @@ def tile_durbinkoopmandisturbancesmootherstep_d1p_kernel(
         k_sc = sbuf("k_sc", [P, P_OBS], U8)
         t_codes = [sbuf("t_codes%d" % g, [P, S], U32) for g in range(2)]
         z_codes = sbuf("z_codes", [P, S], U32)
-        t_sc = sbuf("t_sc", [P, 2, S], U8)
+        t_sc = sbuf("t_sc", [P, S], U8)
         z_sc = sbuf("z_sc", [P, S // 4], U8)
 
         wide, mixed, r_codes, r_planes = {}, {}, {}, {}
@@ -84,13 +84,6 @@ def tile_durbinkoopmandisturbancesmootherstep_d1p_kernel(
                 queue.dma_start(
                     out=plane[32 * q : 32 * q + 4 * groups, :].bitcast(I32),
                     in_=scales[:, 4 * q : 4 * q + 4, :].bitcast(I32),
-                )
-
-        def load_t_planes():
-            for r in range(4):
-                nc.sync.dma_start(
-                    out=t_sc[4 + r : P : 32, :, :].bitcast(I32),
-                    in_=t_scales[:, r:16:4, :].rearrange("g q n -> q g n").bitcast(I32),
                 )
 
         def load_z_planes():
@@ -240,7 +233,7 @@ def tile_durbinkoopmandisturbancesmootherstep_d1p_kernel(
                         nc.tensor.matmul_mx(
                             out=acc[f, b][:, i, :],
                             lhsT=t_codes[g][:, cols].bitcast(FP8X4),
-                            lhsT_scale=t_sc[4:P, g, cols],
+                            lhsT_scale=t_sc[4 * g : P, cols],
                             rhs=r_codes[f, g][:].bitcast(FP8X4),
                             rhs_scale=r_planes[f, g][:],
                             start=(g == 0 and i == 0),
@@ -303,7 +296,7 @@ def tile_durbinkoopmandisturbancesmootherstep_d1p_kernel(
         nc.sync.dma_start(out=rows[0:1, :], in_=finv.rearrange("(o n) -> o n", o=1))
         nc.sync.dma_start(out=rows[32:33, :], in_=h.rearrange("(o n) -> o n", o=1))
         nc.sync.dma_start(out=t_codes[0][:].bitcast(I32), in_=t_dram[0])
-        load_t_planes()
+        load_planes(nc.sync, t_sc, t_scales, 2)
         load_v(0, W)
         nc.sync.dma_start(out=t_codes[1][:].bitcast(I32), in_=t_dram[1])
         load_r(1, 1)

@@ -20,7 +20,9 @@ P = 128
 PACK = 4
 BLOCK = 128
 W = 256
+H = 512
 CHUNKS = M // W
+SLICES = S // P
 
 
 def tile_durbinkoopmandisturbancesmootherstep_d1p_kernel(
@@ -34,19 +36,28 @@ def tile_durbinkoopmandisturbancesmootherstep_d1p_kernel(
 
     with ExitStack() as ctx:
         keep = ctx.enter_context(tc.tile_pool(name="keep", bufs=1))
-        k_psum = ctx.enter_context(tc.psum_pool(name="k_psum", bufs=2))
-        o_psum = ctx.enter_context(tc.psum_pool(name="o_psum", bufs=6))
+        psum = ctx.enter_context(tc.psum_pool(name="psum", bufs=1))
         ctx.enter_context(tc.manual_schedule())
 
         def sbuf(name, shape, dtype):
             return keep.tile(shape, dtype, name=name, align_bytes=256)
 
-        r_raw = {}
+        def bank(i, shape):
+            return psum.tile(shape, F32, name="bank%d" % i)
+
+        r_raw, r_codes, r_planes = {}, {}, {}
+        v_sb, u_codes, u_planes, eps, res = {}, {}, {}, {}, {}
         for half in range(2):
             for g in range(2):
-                r_raw[half, g] = sbuf("r_raw%d_%d" % (half, g), [P, PACK, M // 2], U8)
+                r_raw[half, g] = sbuf("r_raw%d_%d" % (half, g), [P, PACK, H], U8)
+                r_codes[half, g] = sbuf("r_codes%d_%d" % (half, g), [P, H], U32)
+                r_planes[half, g] = sbuf("r_planes%d_%d" % (half, g), [P, H], U8)
+            v_sb[half] = sbuf("v_sb%d" % half, [P, PACK, H], BF16)
+            u_codes[half] = sbuf("u_codes%d" % half, [P, H], U32)
+            u_planes[half] = sbuf("u_planes%d" % half, [P, H], U8)
+            eps[half] = sbuf("eps%d" % half, [P, PACK, H], F32)
+            res[half] = sbuf("res%d" % half, [P, SLICES, H], F32)
         r_sc = sbuf("r_sc", [P, 2, PACK, M // BLOCK], F32)
-        v_sb = sbuf("v_sb", [P, PACK, M], BF16)
         rows = sbuf("rows", [P, P_OBS], BF16)
         pick = sbuf("pick", [P, 2], BF16)
         factors = sbuf("factors", [P, PACK, 2], F32)
@@ -59,30 +70,24 @@ def tile_durbinkoopmandisturbancesmootherstep_d1p_kernel(
         t_sc = sbuf("t_sc", [P, S], U8)
         z_sc = sbuf("z_sc", [P, S // 4], U8)
 
-        wide, mixed, r_codes, r_planes = {}, {}, {}, {}
-        u32, u_mixed, u_codes, u_planes, eps, res = {}, {}, {}, {}, {}, {}
+        wide, paired, mixed, u32, u_mixed = {}, {}, {}, {}, {}
         for f in range(CHUNKS):
             u32[f] = sbuf("u32_%d" % f, [P, PACK, W], F32)
             u_mixed[f] = sbuf("u_mixed%d" % f, [P, W, PACK], BF16)
-            u_codes[f] = sbuf("u_codes%d" % f, [P, W], U32)
-            u_planes[f] = sbuf("u_planes%d" % f, [P, W], U8)
-            eps[f] = sbuf("eps%d" % f, [P, PACK, W], F32)
-            res[f] = sbuf("res%d" % f, [P, S // P, W], F32)
             for g in range(2):
-                if f > 0 and (f, g) != (2, 1):
-                    wide[f, g] = sbuf("wide%d_%d" % (f, g), [P, PACK, W], BF16)
                 mixed[f, g] = sbuf("mixed%d_%d" % (f, g), [P, W, PACK], BF16)
-                r_codes[f, g] = sbuf("r_codes%d_%d" % (f, g), [P, W], U32)
-                r_planes[f, g] = sbuf("r_planes%d_%d" % (f, g), [P, W], U8)
 
         k_dram = k_words.rearrange("g p n t -> p g (n t)").bitcast(I32)
         t_dram = t_words.rearrange("g p n t -> g p (n t)").bitcast(I32)
         z_dram = z_words[0].rearrange("p n t -> p (n t)").bitcast(I32)
 
-        def load_planes(queue, plane, scales, groups):
-            for q in range(4):
+        def in_half(f):
+            return slice(f % 2 * W, (f % 2 + 1) * W)
+
+        def load_planes(queue, plane, scales, quadrants=range(4)):
+            for q in quadrants:
                 queue.dma_start(
-                    out=plane[32 * q : 32 * q + 4 * groups, :].bitcast(I32),
+                    out=plane[32 * q : 32 * q + 8, :].bitcast(I32),
                     in_=scales[:, 4 * q : 4 * q + 4, :].bitcast(I32),
                 )
 
@@ -94,42 +99,45 @@ def tile_durbinkoopmandisturbancesmootherstep_d1p_kernel(
                 )
 
         def load_r(half, g):
-            nc.sync.dma_start(out=r_raw[half, g][:], in_=r_view[:, g, :, half * M // 2 : (half + 1) * M // 2])
+            nc.sync.dma_start(out=r_raw[half, g][:], in_=r_view[:, g, :, half * H : (half + 1) * H])
 
-        def load_v(lo, hi):
-            nc.sync.dma_start(out=v_sb[:, :, lo:hi], in_=v_view[:, :, lo:hi])
+        def load_v(half, cols=slice(0, H)):
+            at = slice(half * H + cols.start, half * H + cols.stop)
+            nc.sync.dma_start(out=v_sb[half][:, :, cols], in_=v_view[:, :, at])
 
-        def widen(f, g, engine, blocks):
+        def load_t(g):
+            nc.sync.dma_start(out=t_codes[g][:].bitcast(I32), in_=t_dram[g])
+
+        def load_rows():
+            nc.sync.dma_start(out=rows[0:1, :], in_=finv.rearrange("(o n) -> o n", o=1))
+            nc.sync.dma_start(out=rows[32:33, :], in_=h.rearrange("(o n) -> o n", o=1))
+
+        def r_block(f, g, i):
+            t, b = divmod(i, W // BLOCK)
+            col = f * W + b * BLOCK
+            src = r_raw[f // 2, g][:, t, col % H : col % H + BLOCK].bitcast(FP8)
+            return t, slice(b * BLOCK, (b + 1) * BLOCK), src, r_sc[:, g, t, col // BLOCK : col // BLOCK + 1]
+
+        def widen(f, g, engine, blocks=range(8)):
+            if (f, g) not in wide:
+                wide[f, g] = sbuf("wide%d_%d" % (f, g), [P, PACK, W], BF16)
             for i in blocks:
-                t, b = divmod(i, W // BLOCK)
-                col = f * W + b * BLOCK
-                at = col % (M // 2)
-                src = r_raw[f // 2, g][:, t, at : at + BLOCK].bitcast(FP8)
-                dst = wide[f, g][:, t, b * BLOCK : (b + 1) * BLOCK]
-                sc = r_sc[:, g, t, col // BLOCK : col // BLOCK + 1]
+                t, cols, src, sc = r_block(f, g, i)
                 if engine == "v":
-                    nc.vector.tensor_scalar(out=dst, in0=src, scalar1=sc, scalar2=None, op0=MULT)
+                    nc.vector.tensor_scalar(out=wide[f, g][:, t, cols], in0=src, scalar1=sc, scalar2=None, op0=MULT)
                 else:
-                    nc.scalar.activation(out=dst, in_=src, func=COPY, scale=sc)
-
-        paired = {}
+                    nc.scalar.activation(out=wide[f, g][:, t, cols], in_=src, func=COPY, scale=sc)
 
         def widen_pairs(f, g, blocks=range(8)):
             if (f, g) not in paired:
                 paired[f, g] = sbuf("paired%d_%d" % (f, g), [P, 2, W, 2], BF16)
             for i in blocks:
-                t, b = divmod(i, W // BLOCK)
-                col = f * W + b * BLOCK
-                at = col % (M // 2)
+                t, cols, src, sc = r_block(f, g, i)
                 nc.vector.tensor_scalar(
-                    out=paired[f, g][:, t // 2, b * BLOCK : (b + 1) * BLOCK, t % 2],
-                    in0=r_raw[f // 2, g][:, t, at : at + BLOCK].bitcast(FP8),
-                    scalar1=r_sc[:, g, t, col // BLOCK : col // BLOCK + 1],
-                    scalar2=None,
-                    op0=MULT,
+                    out=paired[f, g][:, t // 2, cols, t % 2], in0=src, scalar1=sc, scalar2=None, op0=MULT
                 )
 
-        def mix_pairs(f, g, engine="s"):
+        def join(f, g, engine):
             dst = mixed[f, g][:].rearrange("p n t -> p (n t)").bitcast(U32).rearrange("p (n u) -> p n u", u=2)
             src = paired[f, g][:].rearrange("p u n e -> p u (n e)").bitcast(U32).rearrange("p u n -> p n u")
             if engine == "v":
@@ -137,7 +145,7 @@ def tile_durbinkoopmandisturbancesmootherstep_d1p_kernel(
             else:
                 nc.scalar.copy(out=dst, in_=src)
 
-        def mix(f, g, engine="v"):
+        def mix(f, g, engine):
             dst = mixed[f, g][:].rearrange("p (c i) t -> p c t i", i=4)
             src = wide[f, g][:].rearrange("p t (c i) -> p c t i", i=4)
             if engine == "v":
@@ -147,8 +155,8 @@ def tile_durbinkoopmandisturbancesmootherstep_d1p_kernel(
 
         def quant_r(f, g):
             nc.vector.quantize_mx(
-                out=r_codes[f, g][:].bitcast(FP8X4),
-                scales=r_planes[f, g][:],
+                out=r_codes[f // 2, g][:, in_half(f)].bitcast(FP8X4),
+                scales=r_planes[f // 2, g][:, in_half(f)],
                 in_=mixed[f, g][:].rearrange("p n t -> p (n t)"),
             )
 
@@ -157,35 +165,36 @@ def tile_durbinkoopmandisturbancesmootherstep_d1p_kernel(
                 out=k_sc[:].rearrange("p (t m) -> p t m", t=PACK), in_=ks_raw[:].rearrange("p (m t) -> p t m", t=PACK)
             )
 
-        def reorder_k_words(g):
-            nc.vector.tensor_copy(
-                out=k_codes[:, g, :].bitcast(I32).rearrange("p (t m) -> p m t", t=PACK),
-                in_=k_raw[:, g, :].bitcast(I32).rearrange("p (m t) -> p m t", t=PACK),
-            )
+        def reorder_k_words(g, engine):
+            dst = k_codes[:, g, :].rearrange("p (t m) -> p m t", t=PACK)
+            src = k_raw[:, g, :].rearrange("p (m t) -> p m t", t=PACK)
+            if engine == "v":
+                nc.vector.tensor_copy(out=dst.bitcast(I32), in_=src.bitcast(I32))
+            else:
+                nc.scalar.copy(out=dst, in_=src)
 
         kr = {}
 
-        def gain(f, groups=(0, 1)):
-            for g in groups:
-                for t in range(PACK):
-                    if g == 0 and t % 2 == 0:
-                        kr[f, t // 2] = k_psum.tile([P, 2, W], F32, name="k_bank")
-                    cols = slice(t * P, (t + 1) * P)
-                    nc.tensor.matmul_mx(
-                        out=kr[f, t // 2][:, t % 2, :],
-                        lhsT=k_codes[:, g, cols].bitcast(FP8X4),
-                        lhsT_scale=k_sc[4 * g : P, cols],
-                        rhs=r_codes[f, g][:].bitcast(FP8X4),
-                        rhs_scale=r_planes[f, g][:],
-                        start=(g == 0 and t % 2 == 0),
-                        stop=(g == 1 and t % 2 == 1),
-                    )
-
-        def error(f):
+        def gain(f, g, banks=None):
             for t in range(PACK):
+                if g == 0 and t % 2 == 0:
+                    kr[f, t // 2] = bank(banks[t // 2], [P, 2, W])
+                cols = slice(t * P, (t + 1) * P)
+                nc.tensor.matmul_mx(
+                    out=kr[f, t // 2][:, t % 2, :],
+                    lhsT=k_codes[:, g, cols].bitcast(FP8X4),
+                    lhsT_scale=k_sc[4 * g : P, cols],
+                    rhs=r_codes[f // 2, g][:, in_half(f)].bitcast(FP8X4),
+                    rhs_scale=r_planes[f // 2, g][:, in_half(f)],
+                    start=(g == 0 and t % 2 == 0),
+                    stop=(g == 1 and t % 2 == 1),
+                )
+
+        def error(f, ts=range(PACK)):
+            for t in ts:
                 nc.vector.scalar_tensor_tensor(
                     out=u32[f][:, t, :],
-                    in0=v_sb[:, t, f * W : (f + 1) * W],
+                    in0=v_sb[f // 2][:, t, in_half(f)],
                     scalar=factors[:, t, 0:1],
                     in1=kr[f, t // 2][:, t % 2, :],
                     op0=MULT,
@@ -202,205 +211,227 @@ def tile_durbinkoopmandisturbancesmootherstep_d1p_kernel(
 
         def quant_u(f):
             nc.vector.quantize_mx(
-                out=u_codes[f][:].bitcast(FP8X4),
-                scales=u_planes[f][:],
+                out=u_codes[f // 2][:, in_half(f)].bitcast(FP8X4),
+                scales=u_planes[f // 2][:, in_half(f)],
                 in_=u_mixed[f][:].rearrange("p n t -> p (n t)"),
             )
 
         def disturb(f, engine, ts=range(PACK)):
             for t in ts:
-                src, dst = u32[f][:, t, :], eps[f][:, t, :]
+                src, dst = u32[f][:, t, :], eps[f // 2][:, t, in_half(f)]
                 if engine == "v":
                     nc.vector.tensor_scalar(out=dst, in0=src, scalar1=factors[:, t, 1:2], scalar2=None, op0=MULT)
                 else:
                     nc.scalar.activation(out=dst, in_=src, func=COPY, scale=factors[:, t, 1:2])
 
-        def store_eps(f):
-            nc.sync.dma_start(out=eps_view[:, :, f * W : (f + 1) * W], in_=eps[f][:])
+        def store_eps(half, cols=slice(0, H), ts=slice(0, PACK)):
+            at = slice(half * H + cols.start, half * H + cols.stop)
+            nc.sync.dma_start(out=eps_view[:, ts, at], in_=eps[half][:, ts, cols])
+
+        def result_pass(out, s, g, half, cols, start, stop):
+            w = slice(s * P, (s + 1) * P)
+            if g < 2:
+                lhs, lhs_sc = t_codes[g][:, w], t_sc[4 * g : P, w]
+                rhs, rhs_sc = r_codes[half, g][:, cols], r_planes[half, g][:, cols]
+            else:
+                lhs, lhs_sc = z_codes[:, w], z_sc[4 * (s // 2) : P, (s % 2) * P : (s % 2 + 1) * P]
+                rhs, rhs_sc = u_codes[half][:, cols], u_planes[half][:, cols]
+            nc.tensor.matmul_mx(
+                out=out, lhsT=lhs.bitcast(FP8X4), lhsT_scale=lhs_sc, rhs=rhs.bitcast(FP8X4), rhs_scale=rhs_sc,
+                start=start, stop=stop,
+            )
 
         acc = {}
-        pairs = [(0, 1), (2, 3), (4, 5), (6, 7)]
-        groups_of = {f: pairs for f in range(CHUNKS)}
-        groups_of[CHUNKS - 1] = pairs[:3] + [(6,), (7,)]
 
-        def transition(f, banks, groups=(0, 1)):
-            for g in groups:
-                for b in banks:
-                    if g == 0:
-                        acc[f, b] = o_psum.tile([P, len(groups_of[f][b]), W], F32, name="o_bank")
-                    for i, s in enumerate(groups_of[f][b]):
-                        cols = slice(s * P, (s + 1) * P)
-                        nc.tensor.matmul_mx(
-                            out=acc[f, b][:, i, :],
-                            lhsT=t_codes[g][:, cols].bitcast(FP8X4),
-                            lhsT_scale=t_sc[4 * g : P, cols],
-                            rhs=r_codes[f, g][:].bitcast(FP8X4),
-                            rhs_scale=r_planes[f, g][:],
-                            start=(g == 0 and i == 0),
-                            stop=False,
-                        )
+        def wide_pass(half, slices, g, banks=None, cols=slice(0, H)):
+            for i, s in enumerate(slices):
+                first = (half, s) not in acc
+                if first:
+                    acc[half, s] = bank(banks[i], [P, H])
+                result_pass(acc[half, s][:, cols], s, g, half, cols, first, g == 2 and cols.stop == H)
 
-        def observe(f, banks):
-            for b in banks:
-                for i, s in enumerate(groups_of[f][b]):
-                    cols = slice(s * P, (s + 1) * P)
-                    nc.tensor.matmul_mx(
-                        out=acc[f, b][:, i, :],
-                        lhsT=z_codes[:, cols].bitcast(FP8X4),
-                        lhsT_scale=z_sc[4 * (s // 2) : P, (s % 2) * P : (s % 2 + 1) * P],
-                        rhs=u_codes[f][:].bitcast(FP8X4),
-                        rhs_scale=u_planes[f][:],
-                        start=False,
-                        stop=(i == len(groups_of[f][b]) - 1),
-                    )
-
-        def empty(f, b, engine):
-            dst = res[f][:, groups_of[f][b][0] : groups_of[f][b][-1] + 1, :]
+        def empty_wide(half, s, engine):
             if engine == "v":
-                nc.vector.tensor_copy(out=dst, in_=acc[f, b][:])
+                nc.vector.tensor_copy(out=res[half][:, s, :], in_=acc[half, s][:])
             else:
-                nc.scalar.copy(out=dst, in_=acc[f, b][:])
+                nc.scalar.copy(out=res[half][:, s, :], in_=acc[half, s][:])
 
-        def store(f, lo, hi):
-            rows = slice(groups_of[f][lo][0], groups_of[f][hi - 1][-1] + 1)
-            nc.sync.dma_start(out=prev_view[:, rows, f * W : (f + 1) * W], in_=res[f][:, rows, :])
+        def store(half, lo, hi, cols=slice(0, H)):
+            at = slice(half * H + cols.start, half * H + cols.stop)
+            nc.sync.dma_start(out=prev_view[:, lo:hi, at], in_=res[half][:, lo:hi, cols])
 
-        def warm_up(src, n):
-            bank = o_psum.tile([P, 2, W], F32, name="o_bank")
-            src = src[:, 0].rearrange("p n e -> p (n e)")
-            for i in range(n):
-                nc.tensor.matmul(
-                    bank[:].rearrange("p i n -> p (i n)"),
-                    lhsT=src[:, 0:P],
-                    rhs=src,
-                    start=True,
-                    stop=True,
+        pair = {}
+
+        def narrow_pass(f, slices, g, at=None):
+            if g == 0:
+                pair[f, slices[0]] = bank(at, [P, len(slices), W])
+            for i, s in enumerate(slices):
+                result_pass(
+                    pair[f, slices[0]][:, i, :], s, g, f // 2, in_half(f), g == 0 and i == 0, g == 2 and i == len(slices) - 1
                 )
+
+        def empty_narrow(f, slices, engine):
+            dst = res[f // 2][:, slices[0] : slices[-1] + 1, in_half(f)]
+            if engine == "v":
+                nc.vector.tensor_copy(out=dst, in_=pair[f, slices[0]][:])
+            else:
+                nc.scalar.copy(out=dst, in_=pair[f, slices[0]][:])
+
+        def warm_up(first, n):
+            spare_bank = bank(4, [P, H])
+            for i in range(n):
+                nc.tensor.matmul(spare_bank[:], lhsT=first, rhs=zeros[:], start=True, stop=True)
+
+        def spread_factors():
+            spread = bank(5, [P, PACK, 2])
+            for t in range(PACK):
+                nc.tensor.matmul(spread[:, t, :], lhsT=rows[:, t::PACK], rhs=pick[:], start=True, stop=True)
+            nc.scalar.copy(out=factors[:], in_=spread[:])
 
         spare = sbuf("spare", [P, 2], F32)
         nc.vector.memset(spare[:, 0:1], 0.0)
         nc.scalar.activation(out=spare[:, 1:2], in_=spare[:, 0:1], func=COPY)
 
-        nc.vector.memset(rows[:].bitcast(U32), 0)
-        nc.vector.memset(pick[:], 0.0)
-        nc.vector.memset(pick[0:32, 0:1], 1.0)
-        nc.vector.memset(pick[32:64, 1:2], 1.0)
         for plane in (ks_raw, t_sc, z_sc):
             nc.vector.memset(plane[:].bitcast(U32), 0)
-        nc.sync.dma_start(out=r_sc[:], in_=r_scale.rearrange("(g p t) j -> p g t j", p=P, t=PACK))
+        nc.vector.memset(rows[:].bitcast(U32), 0)
+        nc.vector.memset(pick[:], 0.0)
+        zeros = sbuf("zeros", [P, H], BF16)
+        nc.vector.memset(zeros[:].bitcast(U32), 0)
+        nc.vector.memset(pick[0:32, 0:1], 1.0)
+        nc.vector.memset(pick[32:64, 1:2], 1.0)
+
+        def load_r_scales():
+            nc.sync.dma_start(out=r_sc[:], in_=r_scale.rearrange("(g p t) j -> p g t j", p=P, t=PACK))
+
+        def load_k():
+            nc.sync.dma_start(out=k_raw[:].bitcast(I32), in_=k_dram)
+
+        def load_z():
+            nc.sync.dma_start(out=z_codes[:].bitcast(I32), in_=z_dram)
+
+        load_r_scales()
         load_r(0, 0)
         load_r(0, 1)
-        load_planes(nc.sync, ks_raw, k_scales, 2)
-        nc.sync.dma_start(out=k_raw[:].bitcast(I32), in_=k_dram)
+        load_planes(nc.sync, ks_raw, k_scales)
+        load_k()
+        load_rows()
+        load_v(0)
         load_r(1, 0)
-        nc.sync.dma_start(out=rows[0:1, :], in_=finv.rearrange("(o n) -> o n", o=1))
-        nc.sync.dma_start(out=rows[32:33, :], in_=h.rearrange("(o n) -> o n", o=1))
-        nc.sync.dma_start(out=t_codes[0][:].bitcast(I32), in_=t_dram[0])
-        load_planes(nc.sync, t_sc, t_scales, 2)
-        load_v(0, W)
-        nc.sync.dma_start(out=t_codes[1][:].bitcast(I32), in_=t_dram[1])
+        load_planes(nc.sync, t_sc, t_scales)
+        load_t(0)
+        load_t(1)
         load_r(1, 1)
         load_z_planes()
-        nc.sync.dma_start(out=z_codes[:].bitcast(I32), in_=z_dram)
-        load_v(W, 2 * W)
-        load_v(2 * W, M)
+        load_z()
+        load_v(1)
 
         widen_pairs(0, 0)
-        warm_up(paired[0, 0], 2)
-        widen(1, 0, "s", range(8))
-        mix_pairs(0, 0)
+        widen(1, 0, "s")
+        warm_up(wide[1, 0][:, 0, 0:P], 4)
+        join(0, 0, "s")
         widen_pairs(0, 1)
-        warm_up(paired[0, 1], 2)
         widen(1, 1, "s", range(2))
-        mix_pairs(0, 1)
+        join(0, 1, "s")
         widen(1, 1, "s", range(2, 8))
-        widen(2, 0, "s", range(8))
         reorder_k_scales()
         quant_r(0, 0)
-        reorder_k_words(0)
-        reorder_k_words(1)
+        reorder_k_words(0, "v")
+        reorder_k_words(1, "v")
         quant_r(0, 1)
-        gain(0)
-        spread = o_psum.tile([P, PACK, 2], F32, name="o_bank")
-        for t in range(PACK):
-            nc.tensor.matmul(spread[:, t, :], lhsT=rows[:, t::PACK], rhs=pick[:], start=True, stop=True)
-        nc.scalar.copy(out=factors[:], in_=spread[:])
-        widen(3, 0, "s", range(8))
-        transition(0, range(4), (0,))
-        mix(1, 0)
-        mix(1, 1)
+        spread_factors()
+        gain(0, 0, (0, 1))
+        gain(0, 1)
+        mix(1, 0, "v")
+        mix(1, 1, "s")
+        error(0, range(1))
         quant_r(1, 0)
-        transition(1, range(2), (0,))
-        mix(2, 0, "s")
-        error(0)
-        transition(0, range(4), (1,))
-        gain(1, (0,))
-        disturb(0, "s")
-        widen(3, 1, "s", range(2))
+        gain(1, 0, (2, 3))
+        error(0, range(1, 3))
         quant_r(1, 1)
+        gain(1, 1)
+        error(0, range(3, 4))
+        disturb(0, "v", range(2))
+        widen(2, 0, "s")
+        disturb(0, "s", range(2, 4))
         mix_u(0)
-        widen_pairs(2, 1, range(4))
-        store_eps(0)
-        quant_u(0)
-        widen_pairs(2, 1, range(4, 8))
-        quant_r(2, 0)
-        gain(1, (1,))
-        observe(0, range(4))
-        for b in range(4):
-            empty(0, b, "s")
-            store(0, b, b + 1)
-        transition(1, range(2), (1,))
-        for b in range(2, 4):
-            transition(1, (b,))
         error(1)
-        gain(2, (0,))
-        disturb(1, "s", range(4))
-        mix_pairs(2, 1, "v")
+        widen(3, 0, "s", range(4))
+        disturb(1, "s")
+        widen(3, 0, "s", range(4, 8))
+        quant_u(0)
         mix_u(1)
-        quant_r(2, 1)
-        gain(2, (1,))
-        widen(3, 1, "s", range(2, 5))
-        store_eps(1)
+        mix(2, 0, "v")
         quant_u(1)
-        observe(1, range(4))
-        mix(3, 0)
-        widen(3, 1, "v", range(5, 8))
-        for b in range(4):
-            empty(1, b, "s")
-            store(1, b, b + 1)
-        transition(2, (0,))
-        transition(2, (1,))
-        error(2)
+        store_eps(0)
+        for g in range(2):
+            wide_pass(0, range(4), g, (4, 5, 6, 7))
+        for g in range(2):
+            wide_pass(0, (4, 5), g, (0, 1))
+        for g in range(2):
+            wide_pass(0, (6,), g, (2,))
+        wide_pass(0, range(7), 2)
+        quant_r(2, 0)
+        widen_pairs(2, 1)
+        widen(3, 1, "s")
+        mix(3, 0, "v")
+        join(2, 1, "v")
         quant_r(3, 0)
-        disturb(2, "v", range(3, 4))
-        transition(2, (2,))
-        gain(3, (0,))
-        disturb(2, "s", range(3))
-        mix_u(2)
-        mix(3, 1)
-        quant_u(2)
+        quant_r(2, 1)
+        mix(3, 1, "v")
+        for s in range(2):
+            empty_wide(0, s, "s")
+            store(0, s, s + 1)
+        gain(2, 0, (3, 4))
+        for g in range(2):
+            wide_pass(0, (7,), g, (5,))
+        gain(2, 1)
+        wide_pass(0, (7,), 2)
+        for s in range(2, SLICES):
+            empty_wide(0, s, "s")
+            if s % 2 == 1:
+                store(0, s - 1, s + 1)
         quant_r(3, 1)
-        store_eps(2)
-        observe(2, range(1))
-        gain(3, (1,))
-        observe(2, range(1, 3))
-        transition(2, (3,))
-        observe(2, (3,))
-        for b in range(4):
-            empty(2, b, "s")
-            store(2, b, b + 1)
-        for b in range(3):
-            transition(3, (b,))
-        error(3)
+        error(2)
+        gain(3, 0, (6, 7))
+        gain(3, 1)
+        disturb(2, "v", range(2))
+        disturb(2, "s", range(2, 4))
+        store_eps(1, slice(0, W))
+        mix_u(2)
+        error(3, range(1))
+        quant_u(2)
+        error(3, range(1, 4))
+        for b in range(2):
+            for g in range(2):
+                narrow_pass(2, (2 * b, 2 * b + 1), g, b)
+        for g in range(2):
+            wide_pass(1, (4,), g, (2,))
+        for b in range(2):
+            narrow_pass(2, (2 * b, 2 * b + 1), 2)
+            empty_narrow(2, (2 * b, 2 * b + 1), "s")
+            store(1, 2 * b, 2 * b + 2, slice(0, W))
         disturb(3, "v", range(2))
         mix_u(3)
         disturb(3, "v", range(2, 4))
-        store_eps(3)
         quant_u(3)
-        observe(3, range(3))
-        for b in range(3, 5):
-            transition(3, (b,))
-            observe(3, (b,))
-        for b in range(5):
-            empty(3, b, "vs"[b % 2])
-            store(3, b, b + 1)
+        store_eps(1, slice(W, H))
+        for b in range(2):
+            for g in range(2):
+                narrow_pass(3, (2 * b, 2 * b + 1), g, 6 + b)
+        for g in range(2):
+            wide_pass(1, (5,), g, (3,))
+        for b in range(2):
+            narrow_pass(3, (2 * b, 2 * b + 1), 2)
+            empty_narrow(3, (2 * b, 2 * b + 1), "sv"[b])
+        store(1, 0, 4, slice(W, H))
+        wide_pass(1, (4, 5), 2)
+        for s in (6, 7):
+            for g in range(3):
+                wide_pass(1, (s,), g, (s - 2,))
+        for s in range(4, SLICES):
+            empty_wide(1, s, "sv"[s % 2])
+            if s == 5:
+                store(1, 4, 6)
+            if s > 5:
+                store(1, s, s + 1)

@@ -23,6 +23,7 @@ W = 256
 H = 512
 CHUNKS = M // W
 SLICES = S // P
+MIDDLE = CHUNKS
 
 
 def tile_durbinkoopmandisturbancesmootherstep_d1p_kernel(
@@ -45,18 +46,18 @@ def tile_durbinkoopmandisturbancesmootherstep_d1p_kernel(
         def bank(i, shape):
             return psum.tile(shape, F32, name="bank%d" % i)
 
-        r_raw, r_codes, r_planes = {}, {}, {}
-        v_sb, u_codes, u_planes, eps, res = {}, {}, {}, {}, {}
+        r_raw, v_sb, eps = {}, {}, {}
         for half in range(2):
             for g in range(2):
                 r_raw[half, g] = sbuf("r_raw%d_%d" % (half, g), [P, PACK, H], U8)
-                r_codes[half, g] = sbuf("r_codes%d_%d" % (half, g), [P, H], U32)
-                r_planes[half, g] = sbuf("r_planes%d_%d" % (half, g), [P, H], U8)
-            v_sb[half] = sbuf("v_sb%d" % half, [P, PACK, H], BF16)
-            u_codes[half] = sbuf("u_codes%d" % half, [P, H], U32)
-            u_planes[half] = sbuf("u_planes%d" % half, [P, H], U8)
-            eps[half] = sbuf("eps%d" % half, [P, PACK, H], F32)
-            res[half] = sbuf("res%d" % half, [P, SLICES, H], F32)
+        r_codes = [sbuf("r_codes%d" % g, [P, M], U32) for g in range(2)]
+        r_planes = [sbuf("r_planes%d" % g, [P, M], U8) for g in range(2)]
+        u_codes = sbuf("u_codes", [P, M], U32)
+        u_planes = sbuf("u_planes", [P, M], U8)
+        v_sb = sbuf("v_sb", [P, PACK, M], BF16)
+        spans = {f: slice(f * W, (f + 1) * W) for f in range(CHUNKS)}
+        spans[MIDDLE] = slice(W, 3 * W)
+        res = {f: sbuf("res%d" % f, [P, SLICES, at.stop - at.start], F32) for f, at in spans.items()}
         r_sc = sbuf("r_sc", [P, 2, PACK, M // BLOCK], F32)
         rows = sbuf("rows", [P, P_OBS], BF16)
         pick = sbuf("pick", [P, 2], BF16)
@@ -72,6 +73,7 @@ def tile_durbinkoopmandisturbancesmootherstep_d1p_kernel(
 
         wide, paired, mixed, u32, u_mixed = {}, {}, {}, {}, {}
         for f in range(CHUNKS):
+            eps[f] = sbuf("eps%d" % f, [P, PACK, W], F32)
             u32[f] = sbuf("u32_%d" % f, [P, PACK, W], F32)
             u_mixed[f] = sbuf("u_mixed%d" % f, [P, W, PACK], BF16)
             for g in range(2):
@@ -81,8 +83,8 @@ def tile_durbinkoopmandisturbancesmootherstep_d1p_kernel(
         t_dram = t_words.rearrange("g p n t -> g p (n t)").bitcast(I32)
         z_dram = z_words[0].rearrange("p n t -> p (n t)").bitcast(I32)
 
-        def in_half(f):
-            return slice(f % 2 * W, (f % 2 + 1) * W)
+        def chunk(f):
+            return slice(f * W, (f + 1) * W)
 
         def load_planes(queue, plane, scales, quadrants=range(4)):
             for q in quadrants:
@@ -101,9 +103,8 @@ def tile_durbinkoopmandisturbancesmootherstep_d1p_kernel(
         def load_r(half, g):
             nc.sync.dma_start(out=r_raw[half, g][:], in_=r_view[:, g, :, half * H : (half + 1) * H])
 
-        def load_v(half, cols=slice(0, H)):
-            at = slice(half * H + cols.start, half * H + cols.stop)
-            nc.sync.dma_start(out=v_sb[half][:, :, cols], in_=v_view[:, :, at])
+        def load_v(lo, hi):
+            nc.sync.dma_start(out=v_sb[:, :, lo:hi], in_=v_view[:, :, lo:hi])
 
         def load_t(g):
             nc.sync.dma_start(out=t_codes[g][:].bitcast(I32), in_=t_dram[g])
@@ -155,8 +156,8 @@ def tile_durbinkoopmandisturbancesmootherstep_d1p_kernel(
 
         def quant_r(f, g):
             nc.vector.quantize_mx(
-                out=r_codes[f // 2, g][:, in_half(f)].bitcast(FP8X4),
-                scales=r_planes[f // 2, g][:, in_half(f)],
+                out=r_codes[g][:, chunk(f)].bitcast(FP8X4),
+                scales=r_planes[g][:, chunk(f)],
                 in_=mixed[f, g][:].rearrange("p n t -> p (n t)"),
             )
 
@@ -184,8 +185,8 @@ def tile_durbinkoopmandisturbancesmootherstep_d1p_kernel(
                     out=kr[f, t // 2][:, t % 2, :],
                     lhsT=k_codes[:, g, cols].bitcast(FP8X4),
                     lhsT_scale=k_sc[4 * g : P, cols],
-                    rhs=r_codes[f // 2, g][:, in_half(f)].bitcast(FP8X4),
-                    rhs_scale=r_planes[f // 2, g][:, in_half(f)],
+                    rhs=r_codes[g][:, chunk(f)].bitcast(FP8X4),
+                    rhs_scale=r_planes[g][:, chunk(f)],
                     start=(g == 0 and t % 2 == 0),
                     stop=(g == 1 and t % 2 == 1),
                 )
@@ -194,7 +195,7 @@ def tile_durbinkoopmandisturbancesmootherstep_d1p_kernel(
             for t in ts:
                 nc.vector.scalar_tensor_tensor(
                     out=u32[f][:, t, :],
-                    in0=v_sb[f // 2][:, t, in_half(f)],
+                    in0=v_sb[:, t, chunk(f)],
                     scalar=factors[:, t, 0:1],
                     in1=kr[f, t // 2][:, t % 2, :],
                     op0=MULT,
@@ -211,71 +212,56 @@ def tile_durbinkoopmandisturbancesmootherstep_d1p_kernel(
 
         def quant_u(f):
             nc.vector.quantize_mx(
-                out=u_codes[f // 2][:, in_half(f)].bitcast(FP8X4),
-                scales=u_planes[f // 2][:, in_half(f)],
+                out=u_codes[:, chunk(f)].bitcast(FP8X4),
+                scales=u_planes[:, chunk(f)],
                 in_=u_mixed[f][:].rearrange("p n t -> p (n t)"),
             )
 
         def disturb(f, engine, ts=range(PACK)):
             for t in ts:
-                src, dst = u32[f][:, t, :], eps[f // 2][:, t, in_half(f)]
+                src, dst = u32[f][:, t, :], eps[f][:, t, :]
                 if engine == "v":
                     nc.vector.tensor_scalar(out=dst, in0=src, scalar1=factors[:, t, 1:2], scalar2=None, op0=MULT)
                 else:
                     nc.scalar.activation(out=dst, in_=src, func=COPY, scale=factors[:, t, 1:2])
 
-        def store_eps(half, cols=slice(0, H), ts=slice(0, PACK)):
-            at = slice(half * H + cols.start, half * H + cols.stop)
-            nc.sync.dma_start(out=eps_view[:, ts, at], in_=eps[half][:, ts, cols])
-
-        def result_pass(out, s, g, half, cols, start, stop):
-            w = slice(s * P, (s + 1) * P)
-            if g < 2:
-                lhs, lhs_sc = t_codes[g][:, w], t_sc[4 * g : P, w]
-                rhs, rhs_sc = r_codes[half, g][:, cols], r_planes[half, g][:, cols]
-            else:
-                lhs, lhs_sc = z_codes[:, w], z_sc[4 * (s // 2) : P, (s % 2) * P : (s % 2 + 1) * P]
-                rhs, rhs_sc = u_codes[half][:, cols], u_planes[half][:, cols]
-            nc.tensor.matmul_mx(
-                out=out, lhsT=lhs.bitcast(FP8X4), lhsT_scale=lhs_sc, rhs=rhs.bitcast(FP8X4), rhs_scale=rhs_sc,
-                start=start, stop=stop,
-            )
+        def store_eps(f):
+            nc.sync.dma_start(out=eps_view[:, :, chunk(f)], in_=eps[f][:])
 
         acc = {}
 
-        def wide_pass(half, slices, g, banks=None, cols=slice(0, H)):
+        def result(f, slices, g, at=None):
+            cols = spans[f]
+            first = (f, slices) not in acc
+            if first:
+                acc[f, slices] = bank(at, [P, len(slices), cols.stop - cols.start])
             for i, s in enumerate(slices):
-                first = (half, s) not in acc
-                if first:
-                    acc[half, s] = bank(banks[i], [P, H])
-                result_pass(acc[half, s][:, cols], s, g, half, cols, first, g == 2 and cols.stop == H)
-
-        def empty_wide(half, s, engine):
-            if engine == "v":
-                nc.vector.tensor_copy(out=res[half][:, s, :], in_=acc[half, s][:])
-            else:
-                nc.scalar.copy(out=res[half][:, s, :], in_=acc[half, s][:])
-
-        def store(half, lo, hi, cols=slice(0, H)):
-            at = slice(half * H + cols.start, half * H + cols.stop)
-            nc.sync.dma_start(out=prev_view[:, lo:hi, at], in_=res[half][:, lo:hi, cols])
-
-        pair = {}
-
-        def narrow_pass(f, slices, g, at=None):
-            if g == 0:
-                pair[f, slices[0]] = bank(at, [P, len(slices), W])
-            for i, s in enumerate(slices):
-                result_pass(
-                    pair[f, slices[0]][:, i, :], s, g, f // 2, in_half(f), g == 0 and i == 0, g == 2 and i == len(slices) - 1
+                w = slice(s * P, (s + 1) * P)
+                if g < 2:
+                    lhs, lhs_sc = t_codes[g][:, w], t_sc[4 * g : P, w]
+                    rhs, rhs_sc = r_codes[g][:, cols], r_planes[g][:, cols]
+                else:
+                    lhs, lhs_sc = z_codes[:, w], z_sc[4 * (s // 2) : P, (s % 2) * P : (s % 2 + 1) * P]
+                    rhs, rhs_sc = u_codes[:, cols], u_planes[:, cols]
+                nc.tensor.matmul_mx(
+                    out=acc[f, slices][:, i, :],
+                    lhsT=lhs.bitcast(FP8X4),
+                    lhsT_scale=lhs_sc,
+                    rhs=rhs.bitcast(FP8X4),
+                    rhs_scale=rhs_sc,
+                    start=first and i == 0,
+                    stop=g == 2 and i == len(slices) - 1,
                 )
 
-        def empty_narrow(f, slices, engine):
-            dst = res[f // 2][:, slices[0] : slices[-1] + 1, in_half(f)]
+        def empty(f, slices, engine):
+            dst = res[f][:, slices[0] : slices[-1] + 1, :]
             if engine == "v":
-                nc.vector.tensor_copy(out=dst, in_=pair[f, slices[0]][:])
+                nc.vector.tensor_copy(out=dst, in_=acc[f, slices][:])
             else:
-                nc.scalar.copy(out=dst, in_=pair[f, slices[0]][:])
+                nc.scalar.copy(out=dst, in_=acc[f, slices][:])
+
+        def store(f, lo, hi):
+            nc.sync.dma_start(out=prev_view[:, lo:hi, spans[f]], in_=res[f][:, lo:hi, :])
 
         def warm_up(first, n):
             spare_bank = bank(4, [P, H])
@@ -283,10 +269,10 @@ def tile_durbinkoopmandisturbancesmootherstep_d1p_kernel(
                 nc.tensor.matmul(spare_bank[:], lhsT=first, rhs=zeros[:], start=True, stop=True)
 
         def spread_factors():
-            spread = bank(5, [P, PACK, 2])
+            spread = bank(3, [P, PACK, 2])
             for t in range(PACK):
                 nc.tensor.matmul(spread[:, t, :], lhsT=rows[:, t::PACK], rhs=pick[:], start=True, stop=True)
-            nc.scalar.copy(out=factors[:], in_=spread[:])
+            return spread
 
         spare = sbuf("spare", [P, 2], F32)
         nc.vector.memset(spare[:, 0:1], 0.0)
@@ -316,122 +302,131 @@ def tile_durbinkoopmandisturbancesmootherstep_d1p_kernel(
         load_planes(nc.sync, ks_raw, k_scales)
         load_k()
         load_rows()
-        load_v(0)
         load_r(1, 0)
-        load_planes(nc.sync, t_sc, t_scales)
         load_t(0)
+        load_planes(nc.sync, t_sc, t_scales)
+        load_v(0, W)
         load_t(1)
         load_r(1, 1)
         load_z_planes()
         load_z()
-        load_v(1)
+        load_v(W, 2 * W)
+        load_v(2 * W, M)
 
+        pairs = [(0, 1), (2, 3), (4, 5), (6, 7)]
         widen_pairs(0, 0)
         widen(1, 0, "s")
         warm_up(wide[1, 0][:, 0, 0:P], 4)
+        spread = spread_factors()
         join(0, 0, "s")
         widen_pairs(0, 1)
         widen(1, 1, "s", range(2))
         join(0, 1, "s")
         widen(1, 1, "s", range(2, 8))
+        nc.scalar.copy(out=factors[:], in_=spread[:])
+        widen(2, 0, "s")
         reorder_k_scales()
         quant_r(0, 0)
         reorder_k_words(0, "v")
         reorder_k_words(1, "v")
         quant_r(0, 1)
-        spread_factors()
         gain(0, 0, (0, 1))
         gain(0, 1)
+        for b in range(4):
+            result(0, pairs[b], 0, 4 + b)
         mix(1, 0, "v")
-        mix(1, 1, "s")
-        error(0, range(1))
+        mix(1, 1, "v")
         quant_r(1, 0)
         gain(1, 0, (2, 3))
-        error(0, range(1, 3))
+        widen(3, 0, "s", range(2))
+        mix(2, 0, "s")
+        widen(3, 0, "s", range(2, 8))
+        error(0)
+        for b in range(4):
+            result(0, pairs[b], 1)
+        disturb(0, "s")
+        store_eps(0)
+        widen(3, 1, "s", range(2))
         quant_r(1, 1)
         gain(1, 1)
-        error(0, range(3, 4))
-        disturb(0, "v", range(2))
-        widen(2, 0, "s")
-        disturb(0, "s", range(2, 4))
         mix_u(0)
-        error(1)
-        widen(3, 0, "s", range(4))
-        disturb(1, "s")
-        widen(3, 0, "s", range(4, 8))
+        widen_pairs(2, 1, range(4))
         quant_u(0)
-        mix_u(1)
-        mix(2, 0, "v")
-        quant_u(1)
-        store_eps(0)
-        for g in range(2):
-            wide_pass(0, range(4), g, (4, 5, 6, 7))
-        for g in range(2):
-            wide_pass(0, (4, 5), g, (0, 1))
-        for g in range(2):
-            wide_pass(0, (6,), g, (2,))
-        wide_pass(0, range(7), 2)
+        widen_pairs(2, 1, range(4, 8))
         quant_r(2, 0)
-        widen_pairs(2, 1)
-        widen(3, 1, "s")
-        mix(3, 0, "v")
         join(2, 1, "v")
-        quant_r(3, 0)
+        for b in range(4):
+            result(0, pairs[b], 2)
+            empty(0, pairs[b], "s")
+            store(0, 2 * b, 2 * b + 2)
+        gain(2, 0, (0, 1))
+        error(1, range(1))
         quant_r(2, 1)
-        mix(3, 1, "v")
-        for s in range(2):
-            empty_wide(0, s, "s")
-            store(0, s, s + 1)
-        gain(2, 0, (3, 4))
-        for g in range(2):
-            wide_pass(0, (7,), g, (5,))
         gain(2, 1)
-        wide_pass(0, (7,), 2)
-        for s in range(2, SLICES):
-            empty_wide(0, s, "s")
-            if s % 2 == 1:
-                store(0, s - 1, s + 1)
-        quant_r(3, 1)
-        error(2)
-        gain(3, 0, (6, 7))
-        gain(3, 1)
-        disturb(2, "v", range(2))
-        disturb(2, "s", range(2, 4))
-        store_eps(1, slice(0, W))
-        mix_u(2)
-        error(3, range(1))
-        quant_u(2)
-        error(3, range(1, 4))
-        for b in range(2):
+        error(1, range(1, 4))
+        disturb(1, "s")
+        store_eps(1)
+        for f in (1, 2):
             for g in range(2):
-                narrow_pass(2, (2 * b, 2 * b + 1), g, b)
+                result(f, pairs[0], g, 3 + f)
+        for s in range(2, 5):
+            for g in range(2):
+                result(MIDDLE, (s,), g, (6, 7, 2, 3)[s - 2])
+        error(2, range(1))
+        mix_u(1)
+        error(2, range(1, 4))
+        quant_u(1)
+        result(1, pairs[0], 2)
         for g in range(2):
-            wide_pass(1, (4,), g, (2,))
-        for b in range(2):
-            narrow_pass(2, (2 * b, 2 * b + 1), 2)
-            empty_narrow(2, (2 * b, 2 * b + 1), "s")
-            store(1, 2 * b, 2 * b + 2, slice(0, W))
+            result(MIDDLE, (5,), g, 3)
+        mix_u(2)
+        disturb(2, "s", range(2))
+        disturb(2, "v", range(2, 4))
+        store_eps(2)
+        widen(3, 1, "s", range(2, 8))
+        empty(1, pairs[0], "s")
+        store(1, 0, 2)
+        quant_u(2)
+        mix(3, 0, "v")
+        mix(3, 1, "v")
+        quant_r(3, 0)
+        quant_r(3, 1)
+        result(MIDDLE, (6,), 0, 0)
+        result(2, pairs[0], 2)
+        for s in range(2, 6):
+            result(MIDDLE, (s,), 2)
+        empty(2, pairs[0], "s")
+        store(2, 0, 2)
+        gain(3, 0, (1, 4))
+        gain(3, 1)
+        for g in (1, 2):
+            result(MIDDLE, (6,), g)
+        for g in range(3):
+            result(MIDDLE, (7,), g, 5)
+        for s in range(2, SLICES):
+            empty(MIDDLE, (s,), "v" if s in (3, 5) else "s")
+            if s >= 6:
+                store(MIDDLE, s, s + 1)
+            elif s % 2:
+                store(MIDDLE, s - 1, s + 1)
+        error(3)
         disturb(3, "v", range(2))
         mix_u(3)
         disturb(3, "v", range(2, 4))
+        store_eps(3)
         quant_u(3)
-        store_eps(1, slice(W, H))
-        for b in range(2):
+        last = [(0,), (1,), (2, 3), (4, 5), (6,), (7,)]
+        for b in range(4):
             for g in range(2):
-                narrow_pass(3, (2 * b, 2 * b + 1), g, 6 + b)
-        for g in range(2):
-            wide_pass(1, (5,), g, (3,))
-        for b in range(2):
-            narrow_pass(3, (2 * b, 2 * b + 1), 2)
-            empty_narrow(3, (2 * b, 2 * b + 1), "sv"[b])
-        store(1, 0, 4, slice(W, H))
-        wide_pass(1, (4, 5), 2)
-        for s in (6, 7):
+                result(3, last[b], g, (6, 7, 2, 3)[b])
+        for b in range(4):
+            result(3, last[b], 2)
+        for b in range(4, 6):
             for g in range(3):
-                wide_pass(1, (s,), g, (s - 2,))
-        for s in range(4, SLICES):
-            empty_wide(1, s, "sv"[s % 2])
-            if s == 5:
-                store(1, 4, 6)
-            if s > 5:
-                store(1, s, s + 1)
+                result(3, last[b], g, (1, 4)[b - 4])
+        for b in range(4):
+            empty(3, last[b], "vs"[b % 2])
+            store(3, last[b][0], last[b][-1] + 1)
+        empty(3, last[4], "v")
+        empty(3, last[5], "s")
+        store(3, 6, 8)

from contextlib import ExitStack

import concourse.mybir as mybir

S, P_OBS, M = 1024, 512, 1024
FLOPS = 2 * M * (2 * S * P_OBS + S * S)

F32 = mybir.dt.float32
BF16 = mybir.dt.bfloat16
I32 = mybir.dt.int32
U32 = mybir.dt.uint32
U8 = mybir.dt.uint8
FP8 = mybir.dt.float8_e4m3fn
FP8X4 = mybir.dt.float8_e4m3fn_x4
COPY = mybir.ActivationFunctionType.Copy
MULT = mybir.AluOpType.mult
SUB = mybir.AluOpType.subtract

P = 128
PACK = 4
BLOCK = 128
W = 256
H = 512
CHUNKS = M // W
SLICES = S // P
MIDDLE = CHUNKS


def tile_durbinkoopmandisturbancesmootherstep_d1p_kernel(
    tc, r_bytes, r_scale, v, finv, k_words, k_scales, z_words, z_scales, t_words, t_scales, h, out_0, out_1
):
    nc = tc.nc
    r_view = r_bytes.rearrange("(g p t) m -> p g t m", p=P, t=PACK)
    v_view = v.rearrange("(p t) m -> p t m", t=PACK)
    eps_view = out_1.rearrange("(p t) m -> p t m", t=PACK)
    prev_view = out_0.rearrange("(s p) m -> p s m", p=P)

    with ExitStack() as ctx:
        keep = ctx.enter_context(tc.tile_pool(name="keep", bufs=1))
        psum = ctx.enter_context(tc.psum_pool(name="psum", bufs=1))
        ctx.enter_context(tc.manual_schedule())

        def sbuf(name, shape, dtype):
            return keep.tile(shape, dtype, name=name, align_bytes=256)

        def bank(i, shape):
            return psum.tile(shape, F32, name="bank%d" % i)

        r_raw, v_sb, eps = {}, {}, {}
        for half in range(2):
            for g in range(2):
                r_raw[half, g] = sbuf("r_raw%d_%d" % (half, g), [P, PACK, H], U8)
        r_codes = [sbuf("r_codes%d" % g, [P, M], U32) for g in range(2)]
        r_planes = [sbuf("r_planes%d" % g, [P, M], U8) for g in range(2)]
        u_codes = sbuf("u_codes", [P, M], U32)
        u_planes = sbuf("u_planes", [P, M], U8)
        v_sb = sbuf("v_sb", [P, PACK, M], BF16)
        spans = {f: slice(f * W, (f + 1) * W) for f in range(CHUNKS)}
        spans[MIDDLE] = slice(W, 3 * W)
        res = {f: sbuf("res%d" % f, [P, SLICES, at.stop - at.start], F32) for f, at in spans.items()}
        r_sc = sbuf("r_sc", [P, 2, PACK, M // BLOCK], F32)
        rows = sbuf("rows", [P, P_OBS], BF16)
        pick = sbuf("pick", [P, 2], BF16)
        factors = sbuf("factors", [P, PACK, 2], F32)
        k_raw = sbuf("k_raw", [P, 2, P_OBS], U32)
        k_codes = sbuf("k_codes", [P, 2, P_OBS], U32)
        ks_raw = sbuf("ks_raw", [P, P_OBS], U8)
        k_sc = sbuf("k_sc", [P, P_OBS], U8)
        t_codes = [sbuf("t_codes%d" % g, [P, S], U32) for g in range(2)]
        z_codes = sbuf("z_codes", [P, S], U32)
        t_sc = sbuf("t_sc", [P, S], U8)
        z_sc = sbuf("z_sc", [P, S // 4], U8)

        wide, paired, mixed, u32, u_mixed = {}, {}, {}, {}, {}
        for f in range(CHUNKS):
            eps[f] = sbuf("eps%d" % f, [P, PACK, W], F32)
            u32[f] = sbuf("u32_%d" % f, [P, PACK, W], F32)
            u_mixed[f] = sbuf("u_mixed%d" % f, [P, W, PACK], BF16)
            for g in range(2):
                mixed[f, g] = sbuf("mixed%d_%d" % (f, g), [P, W, PACK], BF16)

        k_dram = k_words.rearrange("g p n t -> p g (n t)").bitcast(I32)
        t_dram = t_words.rearrange("g p n t -> g p (n t)").bitcast(I32)
        z_dram = z_words[0].rearrange("p n t -> p (n t)").bitcast(I32)

        def chunk(f):
            return slice(f * W, (f + 1) * W)

        def load_planes(queue, plane, scales, quadrants=range(4)):
            for q in quadrants:
                queue.dma_start(
                    out=plane[32 * q : 32 * q + 8, :].bitcast(I32),
                    in_=scales[:, 4 * q : 4 * q + 4, :].bitcast(I32),
                )

        def load_z_planes():
            for q in range(4):
                nc.sync.dma_start(
                    out=z_sc[32 * q : 32 * q + 16, :].bitcast(I32),
                    in_=z_scales[0, 4 * q : 4 * q + 4, :].bitcast(I32).rearrange("r (j n) -> j r n", j=4),
                )

        def load_r(half, g):
            nc.sync.dma_start(out=r_raw[half, g][:], in_=r_view[:, g, :, half * H : (half + 1) * H])

        def load_v(lo, hi):
            nc.sync.dma_start(out=v_sb[:, :, lo:hi], in_=v_view[:, :, lo:hi])

        def load_t(g):
            nc.sync.dma_start(out=t_codes[g][:].bitcast(I32), in_=t_dram[g])

        def load_rows():
            nc.sync.dma_start(out=rows[0:1, :], in_=finv.rearrange("(o n) -> o n", o=1))
            nc.sync.dma_start(out=rows[32:33, :], in_=h.rearrange("(o n) -> o n", o=1))

        def r_block(f, g, i):
            t, b = divmod(i, W // BLOCK)
            col = f * W + b * BLOCK
            src = r_raw[f // 2, g][:, t, col % H : col % H + BLOCK].bitcast(FP8)
            return t, slice(b * BLOCK, (b + 1) * BLOCK), src, r_sc[:, g, t, col // BLOCK : col // BLOCK + 1]

        def widen(f, g, engine, blocks=range(8)):
            if (f, g) not in wide:
                wide[f, g] = sbuf("wide%d_%d" % (f, g), [P, PACK, W], BF16)
            for i in blocks:
                t, cols, src, sc = r_block(f, g, i)
                if engine == "v":
                    nc.vector.tensor_scalar(out=wide[f, g][:, t, cols], in0=src, scalar1=sc, scalar2=None, op0=MULT)
                else:
                    nc.scalar.activation(out=wide[f, g][:, t, cols], in_=src, func=COPY, scale=sc)

        def widen_pairs(f, g, blocks=range(8)):
            if (f, g) not in paired:
                paired[f, g] = sbuf("paired%d_%d" % (f, g), [P, 2, W, 2], BF16)
            for i in blocks:
                t, cols, src, sc = r_block(f, g, i)
                nc.vector.tensor_scalar(
                    out=paired[f, g][:, t // 2, cols, t % 2], in0=src, scalar1=sc, scalar2=None, op0=MULT
                )

        def join(f, g, engine):
            dst = mixed[f, g][:].rearrange("p n t -> p (n t)").bitcast(U32).rearrange("p (n u) -> p n u", u=2)
            src = paired[f, g][:].rearrange("p u n e -> p u (n e)").bitcast(U32).rearrange("p u n -> p n u")
            if engine == "v":
                nc.vector.tensor_copy(out=dst.bitcast(I32), in_=src.bitcast(I32))
            else:
                nc.scalar.copy(out=dst, in_=src)

        def mix(f, g, engine):
            dst = mixed[f, g][:].rearrange("p (c i) t -> p c t i", i=4)
            src = wide[f, g][:].rearrange("p t (c i) -> p c t i", i=4)
            if engine == "v":
                nc.vector.tensor_copy(out=dst, in_=src)
            else:
                nc.scalar.copy(out=dst, in_=src)

        def quant_r(f, g):
            nc.vector.quantize_mx(
                out=r_codes[g][:, chunk(f)].bitcast(FP8X4),
                scales=r_planes[g][:, chunk(f)],
                in_=mixed[f, g][:].rearrange("p n t -> p (n t)"),
            )

        def reorder_k_scales():
            nc.vector.tensor_copy(
                out=k_sc[:].rearrange("p (t m) -> p t m", t=PACK), in_=ks_raw[:].rearrange("p (m t) -> p t m", t=PACK)
            )

        def reorder_k_words(g, engine):
            dst = k_codes[:, g, :].rearrange("p (t m) -> p m t", t=PACK)
            src = k_raw[:, g, :].rearrange("p (m t) -> p m t", t=PACK)
            if engine == "v":
                nc.vector.tensor_copy(out=dst.bitcast(I32), in_=src.bitcast(I32))
            else:
                nc.scalar.copy(out=dst, in_=src)

        kr = {}

        def gain(f, g, banks=None):
            for t in range(PACK):
                if g == 0 and t % 2 == 0:
                    kr[f, t // 2] = bank(banks[t // 2], [P, 2, W])
                cols = slice(t * P, (t + 1) * P)
                nc.tensor.matmul_mx(
                    out=kr[f, t // 2][:, t % 2, :],
                    lhsT=k_codes[:, g, cols].bitcast(FP8X4),
                    lhsT_scale=k_sc[4 * g : P, cols],
                    rhs=r_codes[g][:, chunk(f)].bitcast(FP8X4),
                    rhs_scale=r_planes[g][:, chunk(f)],
                    start=(g == 0 and t % 2 == 0),
                    stop=(g == 1 and t % 2 == 1),
                )

        def error(f, ts=range(PACK)):
            for t in ts:
                nc.vector.scalar_tensor_tensor(
                    out=u32[f][:, t, :],
                    in0=v_sb[:, t, chunk(f)],
                    scalar=factors[:, t, 0:1],
                    in1=kr[f, t // 2][:, t % 2, :],
                    op0=MULT,
                    op1=SUB,
                )

        def mix_u(f, engine="v"):
            dst = u_mixed[f][:].rearrange("p (c i) t -> p c t i", i=2)
            src = u32[f][:].rearrange("p t (c i) -> p c t i", i=2)
            if engine == "v":
                nc.vector.tensor_copy(out=dst, in_=src)
            else:
                nc.scalar.copy(out=dst, in_=src)

        def quant_u(f):
            nc.vector.quantize_mx(
                out=u_codes[:, chunk(f)].bitcast(FP8X4),
                scales=u_planes[:, chunk(f)],
                in_=u_mixed[f][:].rearrange("p n t -> p (n t)"),
            )

        def disturb(f, engine, ts=range(PACK)):
            for t in ts:
                src, dst = u32[f][:, t, :], eps[f][:, t, :]
                if engine == "v":
                    nc.vector.tensor_scalar(out=dst, in0=src, scalar1=factors[:, t, 1:2], scalar2=None, op0=MULT)
                else:
                    nc.scalar.activation(out=dst, in_=src, func=COPY, scale=factors[:, t, 1:2])

        def store_eps(f):
            nc.sync.dma_start(out=eps_view[:, :, chunk(f)], in_=eps[f][:])

        acc = {}

        def result(f, slices, g, at=None):
            cols = spans[f]
            first = (f, slices) not in acc
            if first:
                acc[f, slices] = bank(at, [P, len(slices), cols.stop - cols.start])
            for i, s in enumerate(slices):
                w = slice(s * P, (s + 1) * P)
                if g < 2:
                    lhs, lhs_sc = t_codes[g][:, w], t_sc[4 * g : P, w]
                    rhs, rhs_sc = r_codes[g][:, cols], r_planes[g][:, cols]
                else:
                    lhs, lhs_sc = z_codes[:, w], z_sc[4 * (s // 2) : P, (s % 2) * P : (s % 2 + 1) * P]
                    rhs, rhs_sc = u_codes[:, cols], u_planes[:, cols]
                nc.tensor.matmul_mx(
                    out=acc[f, slices][:, i, :],
                    lhsT=lhs.bitcast(FP8X4),
                    lhsT_scale=lhs_sc,
                    rhs=rhs.bitcast(FP8X4),
                    rhs_scale=rhs_sc,
                    start=first and i == 0,
                    stop=g == 2 and i == len(slices) - 1,
                )

        def empty(f, slices, engine):
            dst = res[f][:, slices[0] : slices[-1] + 1, :]
            if engine == "v":
                nc.vector.tensor_copy(out=dst, in_=acc[f, slices][:])
            else:
                nc.scalar.copy(out=dst, in_=acc[f, slices][:])

        def store(f, lo, hi):
            nc.sync.dma_start(out=prev_view[:, lo:hi, spans[f]], in_=res[f][:, lo:hi, :])

        def warm_up(first, n):
            spare_bank = bank(4, [P, H])
            for i in range(n):
                nc.tensor.matmul(spare_bank[:], lhsT=first, rhs=zeros[:], start=True, stop=True)

        def spread_factors():
            spread = bank(3, [P, PACK, 2])
            for t in range(PACK):
                nc.tensor.matmul(spread[:, t, :], lhsT=rows[:, t::PACK], rhs=pick[:], start=True, stop=True)
            return spread

        spare = sbuf("spare", [P, 2], F32)
        nc.vector.memset(spare[:, 0:1], 0.0)
        nc.scalar.activation(out=spare[:, 1:2], in_=spare[:, 0:1], func=COPY)

        for plane in (ks_raw, t_sc, z_sc):
            nc.vector.memset(plane[:].bitcast(U32), 0)
        nc.vector.memset(rows[:].bitcast(U32), 0)
        nc.vector.memset(pick[:], 0.0)
        zeros = sbuf("zeros", [P, H], BF16)
        nc.vector.memset(zeros[:].bitcast(U32), 0)
        nc.vector.memset(pick[0:32, 0:1], 1.0)
        nc.vector.memset(pick[32:64, 1:2], 1.0)

        def load_r_scales():
            nc.sync.dma_start(out=r_sc[:], in_=r_scale.rearrange("(g p t) j -> p g t j", p=P, t=PACK))

        def load_k():
            nc.sync.dma_start(out=k_raw[:].bitcast(I32), in_=k_dram)

        def load_z():
            nc.sync.dma_start(out=z_codes[:].bitcast(I32), in_=z_dram)

        load_r_scales()
        load_r(0, 0)
        load_r(0, 1)
        load_planes(nc.sync, ks_raw, k_scales)
        load_k()
        load_rows()
        load_r(1, 0)
        load_t(0)
        load_planes(nc.sync, t_sc, t_scales)
        load_v(0, W)
        load_t(1)
        load_r(1, 1)
        load_z_planes()
        load_z()
        load_v(W, 2 * W)
        load_v(2 * W, M)

        pairs = [(0, 1), (2, 3), (4, 5), (6, 7)]
        widen_pairs(0, 0)
        widen(1, 0, "s")
        warm_up(wide[1, 0][:, 0, 0:P], 4)
        spread = spread_factors()
        join(0, 0, "s")
        widen_pairs(0, 1)
        widen(1, 1, "s", range(2))
        join(0, 1, "s")
        widen(1, 1, "s", range(2, 8))
        nc.scalar.copy(out=factors[:], in_=spread[:])
        widen(2, 0, "s")
        reorder_k_scales()
        quant_r(0, 0)
        reorder_k_words(0, "v")
        reorder_k_words(1, "v")
        quant_r(0, 1)
        gain(0, 0, (0, 1))
        gain(0, 1)
        for b in range(4):
            result(0, pairs[b], 0, 4 + b)
        mix(1, 0, "v")
        mix(1, 1, "v")
        quant_r(1, 0)
        gain(1, 0, (2, 3))
        widen(3, 0, "s", range(2))
        mix(2, 0, "s")
        widen(3, 0, "s", range(2, 8))
        error(0)
        for b in range(4):
            result(0, pairs[b], 1)
        disturb(0, "s")
        store_eps(0)
        widen(3, 1, "s", range(2))
        quant_r(1, 1)
        gain(1, 1)
        mix_u(0)
        widen_pairs(2, 1, range(4))
        quant_u(0)
        widen_pairs(2, 1, range(4, 8))
        quant_r(2, 0)
        join(2, 1, "v")
        for b in range(4):
            result(0, pairs[b], 2)
            empty(0, pairs[b], "s")
            store(0, 2 * b, 2 * b + 2)
        gain(2, 0, (0, 1))
        error(1, range(1))
        quant_r(2, 1)
        gain(2, 1)
        error(1, range(1, 4))
        disturb(1, "s")
        store_eps(1)
        for f in (1, 2):
            for g in range(2):
                result(f, pairs[0], g, 3 + f)
        for s in range(2, 5):
            for g in range(2):
                result(MIDDLE, (s,), g, (6, 7, 2, 3)[s - 2])
        error(2, range(1))
        mix_u(1)
        error(2, range(1, 4))
        quant_u(1)
        result(1, pairs[0], 2)
        for g in range(2):
            result(MIDDLE, (5,), g, 3)
        mix_u(2)
        disturb(2, "s", range(2))
        disturb(2, "v", range(2, 4))
        store_eps(2)
        widen(3, 1, "s", range(2, 8))
        empty(1, pairs[0], "s")
        store(1, 0, 2)
        quant_u(2)
        mix(3, 0, "v")
        mix(3, 1, "v")
        quant_r(3, 0)
        quant_r(3, 1)
        result(MIDDLE, (6,), 0, 0)
        result(2, pairs[0], 2)
        for s in range(2, 6):
            result(MIDDLE, (s,), 2)
        empty(2, pairs[0], "s")
        store(2, 0, 2)
        gain(3, 0, (1, 4))
        gain(3, 1)
        for g in (1, 2):
            result(MIDDLE, (6,), g)
        for g in range(3):
            result(MIDDLE, (7,), g, 5)
        for s in range(2, SLICES):
            empty(MIDDLE, (s,), "v" if s in (3, 5) else "s")
            if s >= 6:
                store(MIDDLE, s, s + 1)
            elif s % 2:
                store(MIDDLE, s - 1, s + 1)
        error(3)
        disturb(3, "v", range(2))
        mix_u(3)
        disturb(3, "v", range(2, 4))
        store_eps(3)
        quant_u(3)
        last = [(0,), (1,), (2, 3), (4, 5), (6,), (7,)]
        for b in range(4):
            for g in range(2):
                result(3, last[b], g, (6, 7, 2, 3)[b])
        for b in range(4):
            result(3, last[b], 2)
        for b in range(4, 6):
            for g in range(3):
                result(3, last[b], g, (1, 4)[b - 4])
        for b in range(4):
            empty(3, last[b], "vs"[b % 2])
            store(3, last[b][0], last[b][-1] + 1)
        empty(3, last[4], "v")
        empty(3, last[5], "s")
        store(3, 6, 8)
